import numpy as np
import ml_dtypes


def mxq(x, axis, fmt="e4m3"):
    dtype, down = {"e4m3": (ml_dtypes.float8_e4m3fn, 7), "e5m2": (ml_dtypes.float8_e5m2, 14)}[fmt]
    v = np.moveaxis(np.asarray(x, np.float32).astype(ml_dtypes.bfloat16).astype(np.float64), axis, -1)
    blocks = v.reshape(v.shape[:-1] + (-1, 32))
    amax = np.abs(blocks).max(-1, keepdims=True)
    byte = np.maximum(np.where(amax > 0, np.frexp(amax)[1] - 1 + 127, 0) - down, 1)
    scale = np.exp2(byte - 127.0)
    codes = (blocks / scale).astype(np.float32).astype(dtype).astype(np.float64)
    return np.moveaxis((codes * scale).reshape(v.shape), -1, axis)


WIDE = False


def mx_kscale(k):
    if not WIDE:
        return np.ones(k)
    levels = np.array([10, -10, 5, -5, 0])
    if k % 512:
        return np.exp2(np.random.permutation(np.resize(levels, k // 32))).repeat(32)
    a = np.empty((k // 512, 16))
    for p in range(k // 512):
        a[p, :8] = np.random.permutation(np.resize(levels, 8))
        for g in range(8):
            far = levels[np.abs(levels - a[p, g]) >= 10]
            a[p, g + 8] = far[np.random.randint(len(far))]
    return np.exp2(a.ravel()).repeat(32)


def f64(x):
    return np.asarray(x).astype(np.float64)


def striped(idx):
    return np.tile(idx.reshape(-1, 16).T, (8, 1)).astype(np.uint16)


def unstriped(offs):
    return offs[:16].T.reshape(-1).astype(np.int64)


E2M1 = np.array([0.0, 0.5, 1.0, 1.5, 2.0, 3.0, 4.0, 6.0, -0.0, -0.5, -1.0, -1.5, -2.0, -3.0, -4.0, -6.0])


def pack_weight(w, fmt):
    k, n = w.shape
    w = f64(np.asarray(w, np.float32).astype(ml_dtypes.bfloat16)).reshape(k // 32, 32, n)
    amax = np.abs(w).max(1)
    if fmt == "e4m3":
        byte = np.frexp(amax)[1] - 1 + 127 - 7
    else:
        mant, ex = np.frexp(amax / 6.0)
        byte = np.where(mant > 0.5, ex, ex - 1) + 127
    byte = np.clip(np.where(amax > 0, byte, 1), 1, 254)
    scaled = (w * np.exp2(127.0 - byte)[:, None, :]).reshape(k, n).astype(np.float32)
    by_word = np.ascontiguousarray(scaled.reshape(k // 512, 128, 4, n).transpose(0, 1, 3, 2))
    if fmt == "e4m3":
        words = by_word.astype(ml_dtypes.float8_e4m3fn).view(np.uint8)
    else:
        c = by_word.astype(ml_dtypes.float4_e2m1fn).view(np.uint8) & 0xF
        words = (c[..., 0::2] | (c[..., 1::2] << 4)).reshape(k // 512, 128, 2 * n)
    return np.ascontiguousarray(words), np.ascontiguousarray(byte.astype(np.uint8).reshape(k // 512, 16, n))


def unpack_weight(words, scales, fmt):
    g, _, n = scales.shape
    words = np.ascontiguousarray(words).reshape(g, 128, n, -1)
    if fmt == "e4m3":
        vals = words.view(ml_dtypes.float8_e4m3fn).astype(np.float64)
    else:
        nib = np.empty((g, 128, n, 4), np.uint8)
        nib[..., 0::2] = words & 0xF
        nib[..., 1::2] = words >> 4
        vals = E2M1[nib]
    vals = vals * np.repeat(np.exp2(scales.astype(np.float64) - 127.0), 8, axis=1)[..., None]
    return vals.transpose(0, 1, 3, 2).reshape(g * 512, n)


def silu(v):
    return v / (1.0 + np.exp(-np.maximum(v, -700.0)))


K, T, E, C, H, N = 512, 768, 18, 128, 512, 128
TOP = 3


def by_expert(wq, xq):
    return np.concatenate([wq[e].T @ xq[:, e * C:(e + 1) * C] for e in range(E)], axis=1)


def setup_inputs():
    n = np.random.standard_normal
    s = mx_kscale(K)[:, None]
    u = mx_kscale(H)
    deal = np.repeat(np.arange(E), C).reshape(TOP, T)[:, np.random.permutation(T)]
    deal = np.take_along_axis(deal, np.argsort(np.random.rand(TOP, T), axis=0), axis=0)
    for _ in range(8):
        s_, t_ = np.random.permutation(T).reshape(2, -1); r = np.random.randint(TOP, size=T // 2); x, y = deal[r, s_].copy(), deal[r, t_].copy()
        ok = ~((deal[:, s_] == y).any(0) | (deal[:, t_] == x).any(0)); deal[r[ok], s_[ok]] = y[ok]; deal[r[ok], t_[ok]] = x[ok]
    order = np.lexsort((np.random.rand(TOP * T), deal.reshape(-1)))
    slot_token = order % T; pos = np.empty(TOP * T, np.int64); pos[order] = np.arange(TOP * T); pos = pos.reshape(TOP, T)
    g = np.random.uniform(0.5, 1.5, (TOP, T)); g = g / g.sum(0)
    x = pack_weight(n((K, T)) * s, "e4m3")
    return {
        "x_words": x[0],
        "x_scales": x[1],
        "w1": (n((E, K, H)) / np.sqrt(K) / s[None]).astype(np.float32),
        "w3": (n((E, K, H)) / np.sqrt(K) / s[None] * u[None, None, :]).astype(np.float32),
        "w2": (n((E, H, N)) / np.sqrt(H) / u[None, :, None]).astype(np.float32),
        "gate": np.stack([np.tile(r, (N, 1)) for r in g]).astype(np.float32),
        "offs": striped(slot_token),
        "pos1": striped(pos[0]),
        "pos2": striped(pos[1]),
        "pos3": striped(pos[2]),
    }


def reference(x_words, x_scales, w1, w3, w2, gate, offs, pos1, pos2, pos3):
    idx = unstriped(offs)
    xq = unpack_weight(x_words, x_scales, "e4m3")[:, idx]
    h = silu(by_expert(mxq(f64(w1), 1, "e4m3"), xq))
    h = h * by_expert(mxq(f64(w3), 1, "e4m3"), xq)
    y = by_expert(mxq(f64(w2), 1, "e4m3"), mxq(h, 0, "e4m3"))
    return sum(f64(gate[r]) * y[:, unstriped(p)] for r, p in enumerate((pos1, pos2, pos3)))

@@ -1,0 +1,181 @@
+from contextlib import ExitStack
+
+import concourse.mybir as mybir
+
+K, T, E, C, H, N = 512, 768, 18, 128, 512, 128
+TOP = 3
+S = E * C
+FLOPS = 2 * S * (2 * K * H + H * N)
+
+F32 = mybir.dt.float32
+BF16 = mybir.dt.bfloat16
+I32 = mybir.dt.int32
+U32 = mybir.dt.uint32
+U16 = mybir.dt.uint16
+U8 = mybir.dt.uint8
+FP8X4 = mybir.dt.float8_e4m3fn_x4
+MULT = mybir.AluOpType.mult
+ADD = mybir.AluOpType.add
+SILU = mybir.ActivationFunctionType.Silu
+
+P = 128
+PACK = 4
+LIST_ROWS = 16
+GATHER_EXPERTS = 3
+LATE_FROM = 9
+LAST_SPLIT = 64
+STREAM_BUFS = 14
+TOKEN_CHUNKS = ((0, 512), (512, 768))
+
+
+def tile_moe_pkd_glu_silu_kernel(
+    tc, x_words, x_scales, w1, w3, w2, gate, offs, pos1, pos2, pos3, out
+):
+    nc = tc.nc
+    with ExitStack() as ctx:
+        keep = ctx.enter_context(tc.tile_pool(name="keep", bufs=1))
+        stream = ctx.enter_context(tc.tile_pool(name="stream", bufs=STREAM_BUFS))
+        work = ctx.enter_context(tc.tile_pool(name="work", bufs=3))
+        psum = ctx.enter_context(tc.psum_pool(name="psum", bufs=2))
+
+        slot_list = keep.tile([P, S // LIST_ROWS], U16, name="slot_list")
+        nc.sync.dma_start(slot_list[:], offs)
+        token_words = keep.tile([P, T], I32, name="token_words")
+        nc.sync.dma_start(token_words[:], x_words[0].rearrange("p t r -> p (t r)").bitcast(I32))
+        token_scales = keep.tile([P, T // 4], I32, name="token_scales")
+        nc.vector.memset(token_scales[:], 0)
+        for q in range(4):
+            nc.sync.dma_start(
+                token_scales[32 * q : 32 * q + 4, :],
+                x_scales[0, 4 * q : 4 * q + 4, :].bitcast(I32),
+            )
+        y = keep.tile([P, S], F32, name="y")
+
+        def load(matrix, width):
+            raw = stream.tile([P, PACK, width], F32, name="raw", tag="raw")
+            nc.sync.dma_start(raw[:], matrix.rearrange("(p j) c -> p j c", j=PACK))
+            return raw
+
+        def gather_tokens(g):
+            width = GATHER_EXPERTS * C
+            offsets = slot_list[:, g * width // LIST_ROWS : (g + 1) * width // LIST_ROWS]
+            words = work.tile([P, width], U32, name="slot_words", align_bytes=64)
+            scales = work.tile([P, width], U8, name="slot_scales", align_bytes=64)
+            nc.vector.tensor_copy(words[:], token_words[:].bitcast(U32).indirect(offsets))
+            nc.vector.tensor_copy(scales[:], token_scales[:].bitcast(U8).indirect(offsets))
+            return words, scales
+
+        def quantize(pool, rounded, width, name):
+            codes = pool.tile([P, width], U32, name=name + "_codes", align_bytes=64)
+            scales = pool.tile([P, width], U8, name=name + "_scales", align_bytes=64)
+            nc.vector.quantize_mx(out=codes[:].bitcast(FP8X4), scales=scales[:], in_=rounded[:])
+            return codes, scales
+
+        def round_first(raw, name, shares):
+            rounded = work.tile([P, H * PACK], BF16, name=name, align_bytes=64)
+            dst = rounded[:].rearrange("p (t m j) -> p m j t", t=PACK, j=PACK)
+            src = raw[:].rearrange("p j (m t) -> p m j t", t=PACK)
+            for copy, m0, m1 in shares:
+                copy(dst[:, m0:m1], src[:, m0:m1])
+            return rounded
+
+        def first_product(weights, tokens, e, name):
+            cols = slice((e % GATHER_EXPERTS) * C, (e % GATHER_EXPERTS + 1) * C)
+            acc = psum.tile([P, PACK, C], F32, name=name)
+            for t in range(PACK):
+                nc.tensor.matmul_mx(
+                    out=acc[:, t, :],
+                    lhsT=weights[0][:, t * P : (t + 1) * P].bitcast(FP8X4),
+                    lhsT_scale=weights[1][:, t * P : (t + 1) * P],
+                    rhs=tokens[0][:, cols].bitcast(FP8X4),
+                    rhs_scale=tokens[1][:, cols],
+                    start=True,
+                    stop=True,
+                )
+            return acc
+
+        def hidden(e, raw1, raw3, tokens):
+            rounded1 = round_first(raw1, "rounded1", [(nc.vector.tensor_copy, 0, P)])
+            a = first_product(quantize(work, rounded1, H, "w1"), tokens, e, "a")
+            if e < E - 1:
+                shares = [(nc.scalar.copy, 0, P)]
+            else:
+                shares = [(nc.scalar.copy, 0, LAST_SPLIT), (nc.vector.tensor_copy, LAST_SPLIT, P)]
+            rounded3 = round_first(raw3, "rounded3", shares)
+            b = first_product(quantize(work, rounded3, H, "w3"), tokens, e, "b")
+            silu_a = work.tile([P, C, PACK], F32, name="silu_a")
+            nc.scalar.activation(silu_a[:], a[:].rearrange("p t c -> p c t"), SILU)
+            h = work.tile([P, C * PACK], BF16, name="h", align_bytes=64)
+            nc.vector.tensor_tensor(
+                h[:].rearrange("p (c t) -> p c t", t=PACK), b[:].rearrange("p t c -> p c t"), silu_a[:], MULT
+            )
+            return quantize(keep, h, C, "h%d" % e)
+
+        def load_second(experts):
+            raw = stream.tile([P, len(experts), PACK, N], F32, name="raw", tag="raw")
+            nc.sync.dma_start(
+                raw[:], w2[experts[0] : experts[-1] + 1].rearrange("g (p j) c -> p g j c", j=PACK)
+            )
+            return raw
+
+        def second_product(experts, raw2, copy):
+            count = len(experts)
+            rounded2 = work.tile([P, count * N * PACK], BF16, name="rounded2", align_bytes=64)
+            for g in range(count):
+                copy(
+                    rounded2[:, g * N * PACK : (g + 1) * N * PACK].rearrange("p (m i j) -> p m j i", i=PACK, j=PACK),
+                    raw2[:, g].rearrange("p j (m i) -> p m j i", i=PACK),
+                )
+            codes, scales = quantize(work, rounded2, count * N, "w2")
+            acc = psum.tile([P, count * C], F32, name="y_acc")
+            for g, e in enumerate(experts):
+                nc.tensor.matmul_mx(
+                    out=acc[:, g * C : (g + 1) * C],
+                    lhsT=codes[:, g * N : (g + 1) * N].bitcast(FP8X4),
+                    lhsT_scale=scales[:, g * N : (g + 1) * N],
+                    rhs=h_mx[e][0][:].bitcast(FP8X4),
+                    rhs_scale=h_mx[e][1][:],
+                    start=True,
+                    stop=True,
+                )
+            nc.scalar.copy(y[:, experts[0] * C : (experts[-1] + 1) * C], acc[:])
+
+        late_groups = [(e, e + 1) for e in range(LATE_FROM, E - 1, 2)] + [(E - 1,)]
+        back_lists = []
+        h_mx = {}
+        for e in range(E):
+            raw1 = load(w1[e], H)
+            raw3 = load(w3[e], H)
+            if e < LATE_FROM:
+                raw2 = load_second((e,))
+            if e == 0:
+                for r, pos in enumerate((pos1, pos2, pos3)):
+                    back = keep.tile([P, T // LIST_ROWS], U16, name="back_list%d" % r)
+                    nc.sync.dma_start(back[:], pos)
+                    back_lists.append(back)
+            if e % GATHER_EXPERTS == 0:
+                tokens = gather_tokens(e // GATHER_EXPERTS)
+            if e == E - 1:
+                late_raw2 = [load_second(group) for group in late_groups]
+                gates = []
+                for t0, t1 in TOKEN_CHUNKS:
+                    chunk = stream.tile([P, TOP, t1 - t0], F32, name="gates", tag="raw")
+                    nc.sync.dma_start(chunk[:], gate[:, :, t0:t1].rearrange("r p t -> p r t"))
+                    gates.append(chunk)
+            h_mx[e] = hidden(e, raw1, raw3, tokens)
+            if e < LATE_FROM:
+                second_product((e,), raw2, nc.scalar.copy)
+        for g, group in enumerate(late_groups):
+            second_product(group, late_raw2[g], nc.vector.tensor_copy if g in (1, 4) else nc.scalar.copy)
+
+        for c, (t0, t1) in enumerate(TOKEN_CHUNKS):
+            width = t1 - t0
+            parts = [keep.tile([P, width], F32, name="part%d_%d" % (r, t0)) for r in range(TOP)]
+            pair = keep.tile([P, width], F32, name="pair%d" % t0)
+            total = keep.tile([P, width], F32, name="total%d" % t0)
+            for r in range(TOP):
+                offsets = back_lists[r][:, t0 // LIST_ROWS : t1 // LIST_ROWS]
+                nc.vector.tensor_tensor(parts[r][:], y[:].indirect(offsets), gates[c][:, r, :], MULT)
+            nc.vector.tensor_tensor(pair[:], parts[0][:], parts[1][:], ADD)
+            nc.vector.tensor_tensor(total[:], pair[:], parts[2][:], ADD)
+            nc.sync.dma_start(out[:, t0:t1], total[:])

@@ -23,9 +23,13 @@ PACK = 4
 LIST_ROWS = 16
 GATHER_EXPERTS = 3
 LATE_FROM = 9
-LAST_SPLIT = 64
-STREAM_BUFS = 14
-TOKEN_CHUNKS = ((0, 512), (512, 768))
+LAST_SPLIT = 48
+SINGLES_FROM = 0
+EARLY_W2 = {0: (0,), 1: (1, 2, 3, 4), 5: (5, 6, 7, 8)}
+STREAM_BUFS = 12
+H_AT = 256
+W2_AT = 1024
+TOKEN_CHUNKS = ((0, 576), (576, 768))
 
 
 def tile_moe_pkd_glu_silu_kernel(
@@ -37,24 +41,20 @@ def tile_moe_pkd_glu_silu_kernel(
         stream = ctx.enter_context(tc.tile_pool(name="stream", bufs=STREAM_BUFS))
         work = ctx.enter_context(tc.tile_pool(name="work", bufs=3))
         psum = ctx.enter_context(tc.psum_pool(name="psum", bufs=2))
+        late_psum = ctx.enter_context(tc.psum_pool(name="late_psum", bufs=1))
 
-        slot_list = keep.tile([P, S // LIST_ROWS], U16, name="slot_list")
-        nc.sync.dma_start(slot_list[:], offs)
-        token_words = keep.tile([P, T], I32, name="token_words")
-        nc.sync.dma_start(token_words[:], x_words[0].rearrange("p t r -> p (t r)").bitcast(I32))
-        token_scales = keep.tile([P, T // 4], I32, name="token_scales")
-        nc.vector.memset(token_scales[:], 0)
-        for q in range(4):
-            nc.sync.dma_start(
-                token_scales[32 * q : 32 * q + 4, :],
-                x_scales[0, 4 * q : 4 * q + 4, :].bitcast(I32),
-            )
         y = keep.tile([P, S], F32, name="y")
 
-        def load(matrix, width):
-            raw = stream.tile([P, PACK, width], F32, name="raw", tag="raw")
-            nc.sync.dma_start(raw[:], matrix.rearrange("(p j) c -> p j c", j=PACK))
-            return raw
+        first_stage = [keep.tile([P, H * PACK], BF16, name="stage1_%d" % i, align_bytes=64) for i in range(2)]
+        third_stage = [keep.tile([P, H * PACK], BF16, name="stage3_%d" % i, align_bytes=64) for i in range(1)]
+        late_stage = [keep.tile([P, H * PACK], BF16, name="late_stage%d" % i, align_bytes=64) for i in range(2)]
+
+        def load(weights, experts, pool=stream, name="raw"):
+            raw = pool.tile([P, len(experts), PACK, weights.shape[2]], F32, name=name)
+            nc.sync.dma_start(
+                raw[:], weights[experts[0] : experts[-1] + 1].rearrange("g (p j) c -> p g j c", j=PACK)
+            )
+            return {e: raw[:, g] for g, e in enumerate(experts)}
 
         def gather_tokens(g):
             width = GATHER_EXPERTS * C
@@ -68,16 +68,14 @@ def tile_moe_pkd_glu_silu_kernel(
         def quantize(pool, rounded, width, name):
             codes = pool.tile([P, width], U32, name=name + "_codes", align_bytes=64)
             scales = pool.tile([P, width], U8, name=name + "_scales", align_bytes=64)
-            nc.vector.quantize_mx(out=codes[:].bitcast(FP8X4), scales=scales[:], in_=rounded[:])
+            nc.vector.quantize_mx(out=codes[:].bitcast(FP8X4), scales=scales[:], in_=rounded)
             return codes, scales
 
-        def round_first(raw, name, shares):
-            rounded = work.tile([P, H * PACK], BF16, name=name, align_bytes=64)
-            dst = rounded[:].rearrange("p (t m j) -> p m j t", t=PACK, j=PACK)
-            src = raw[:].rearrange("p j (m t) -> p m j t", t=PACK)
+        def round_first(raw, rounded, shares):
+            dst = rounded.rearrange("p (t m j) -> p m j t", t=PACK, j=PACK)
+            src = raw.rearrange("p j (m t) -> p m j t", t=PACK)
             for copy, m0, m1 in shares:
                 copy(dst[:, m0:m1], src[:, m0:m1])
-            return rounded
 
         def first_product(weights, tokens, e, name):
             cols = slice((e % GATHER_EXPERTS) * C, (e % GATHER_EXPERTS + 1) * C)
@@ -94,43 +92,36 @@ def tile_moe_pkd_glu_silu_kernel(
                 )
             return acc
 
-        def hidden(e, raw1, raw3, tokens):
-            rounded1 = round_first(raw1, "rounded1", [(nc.vector.tensor_copy, 0, P)])
-            a = first_product(quantize(work, rounded1, H, "w1"), tokens, e, "a")
+        def hidden(e, tokens):
+            stage = first_stage[e % 2]
+            round_first(raw1[e], stage[:], [(nc.vector.tensor_copy, 0, P)])
+            a = first_product(quantize(work, stage[:], H, "w1"), tokens, e, "a")
             if e < E - 1:
                 shares = [(nc.scalar.copy, 0, P)]
             else:
                 shares = [(nc.scalar.copy, 0, LAST_SPLIT), (nc.vector.tensor_copy, LAST_SPLIT, P)]
-            rounded3 = round_first(raw3, "rounded3", shares)
-            b = first_product(quantize(work, rounded3, H, "w3"), tokens, e, "b")
-            silu_a = work.tile([P, C, PACK], F32, name="silu_a")
+            round_first(raw3[e], third_stage[0][:], shares)
+            b = first_product(quantize(work, third_stage[0][:], H, "w3"), tokens, e, "b")
+            silu_a = work.tile([P, C, PACK], F32, name="silu_a", bufs=2)
             nc.scalar.activation(silu_a[:], a[:].rearrange("p t c -> p c t"), SILU)
-            h = work.tile([P, C * PACK], BF16, name="h", align_bytes=64)
+            h = stage[:, H_AT : H_AT + C * PACK]
             nc.vector.tensor_tensor(
-                h[:].rearrange("p (c t) -> p c t", t=PACK), b[:].rearrange("p t c -> p c t"), silu_a[:], MULT
+                h.rearrange("p (c t) -> p c t", t=PACK), b[:].rearrange("p t c -> p c t"), silu_a[:], MULT
             )
             return quantize(keep, h, C, "h%d" % e)
 
-        def load_second(experts):
-            raw = stream.tile([P, len(experts), PACK, N], F32, name="raw", tag="raw")
-            nc.sync.dma_start(
-                raw[:], w2[experts[0] : experts[-1] + 1].rearrange("g (p j) c -> p g j c", j=PACK)
-            )
-            return raw
-
-        def second_product(experts, raw2, copy):
+        def second_product(experts, copies, stage, at, places):
             count = len(experts)
-            rounded2 = work.tile([P, count * N * PACK], BF16, name="rounded2", align_bytes=64)
-            for g in range(count):
-                copy(
+            rounded2 = stage[:, at : at + count * N * PACK]
+            for g, e in enumerate(experts):
+                copies[g](
                     rounded2[:, g * N * PACK : (g + 1) * N * PACK].rearrange("p (m i j) -> p m j i", i=PACK, j=PACK),
-                    raw2[:, g].rearrange("p j (m i) -> p m j i", i=PACK),
+                    raw2[e].rearrange("p j (m i) -> p m j i", i=PACK),
                 )
             codes, scales = quantize(work, rounded2, count * N, "w2")
-            acc = psum.tile([P, count * C], F32, name="y_acc")
             for g, e in enumerate(experts):
                 nc.tensor.matmul_mx(
-                    out=acc[:, g * C : (g + 1) * C],
+                    out=places[g],
                     lhsT=codes[:, g * N : (g + 1) * N].bitcast(FP8X4),
                     lhsT_scale=scales[:, g * N : (g + 1) * N],
                     rhs=h_mx[e][0][:].bitcast(FP8X4),
@@ -138,16 +129,36 @@ def tile_moe_pkd_glu_silu_kernel(
                     start=True,
                     stop=True,
                 )
-            nc.scalar.copy(y[:, experts[0] * C : (experts[-1] + 1) * C], acc[:])
 
-        late_groups = [(e, e + 1) for e in range(LATE_FROM, E - 1, 2)] + [(E - 1,)]
+        on_scalar, on_vector = nc.scalar.copy, nc.vector.tensor_copy
+        late_groups = [
+            ((9, 10), (on_vector, on_vector), late_stage[0], 0),
+            ((11, 12), (on_scalar, on_scalar), late_stage[0], 1024),
+            ((13, 14), (on_scalar, on_scalar), late_stage[1], 0),
+            ((15, 16), (on_vector, on_vector), late_stage[1], 1024),
+            ((17,), (on_scalar,), first_stage[0], 0),
+        ]
         back_lists = []
-        h_mx = {}
+        raw1, raw3, raw2, h_mx = {}, {}, {}, {}
+        raw1.update(load(w1, (0,)))
+        slot_list = keep.tile([P, S // LIST_ROWS], U16, name="slot_list")
+        nc.sync.dma_start(slot_list[:], offs)
+        token_words = keep.tile([P, T], I32, name="token_words")
+        nc.sync.dma_start(token_words[:], x_words[0].rearrange("p t r -> p (t r)").bitcast(I32))
+        token_scales = keep.tile([P, T // 4], I32, name="token_scales")
+        nc.vector.memset(token_scales[:], 0)
+        for q in range(4):
+            nc.sync.dma_start(
+                token_scales[32 * q : 32 * q + 4, :],
+                x_scales[0, 4 * q : 4 * q + 4, :].bitcast(I32),
+            )
         for e in range(E):
-            raw1 = load(w1[e], H)
-            raw3 = load(w3[e], H)
-            if e < LATE_FROM:
-                raw2 = load_second((e,))
+            if e not in raw1:
+                raw1.update(load(w1, (e, e + 1) if e < SINGLES_FROM - 1 else (e,)))
+            if e in EARLY_W2:
+                raw2.update(load(w2, EARLY_W2[e]))
+            if e not in raw3:
+                raw3.update(load(w3, (e, e + 1) if e < SINGLES_FROM - 1 else (e,)))
             if e == 0:
                 for r, pos in enumerate((pos1, pos2, pos3)):
                     back = keep.tile([P, T // LIST_ROWS], U16, name="back_list%d" % r)
@@ -156,17 +167,28 @@ def tile_moe_pkd_glu_silu_kernel(
             if e % GATHER_EXPERTS == 0:
                 tokens = gather_tokens(e // GATHER_EXPERTS)
             if e == E - 1:
-                late_raw2 = [load_second(group) for group in late_groups]
+                for group in late_groups:
+                    raw2.update(load(w2, group[0]))
                 gates = []
                 for t0, t1 in TOKEN_CHUNKS:
                     chunk = stream.tile([P, TOP, t1 - t0], F32, name="gates", tag="raw")
                     nc.sync.dma_start(chunk[:], gate[:, :, t0:t1].rearrange("r p t -> p r t"))
                     gates.append(chunk)
-            h_mx[e] = hidden(e, raw1, raw3, tokens)
+            h_mx[e] = hidden(e, tokens)
             if e < LATE_FROM:
-                second_product((e,), raw2, nc.scalar.copy)
-        for g, group in enumerate(late_groups):
-            second_product(group, late_raw2[g], nc.vector.tensor_copy if g in (1, 4) else nc.scalar.copy)
+                acc = psum.tile([P, C], F32, name="y_acc")
+                second_product((e,), (on_scalar,), first_stage[e % 2], W2_AT, [acc[:]])
+                nc.scalar.copy(y[:, e * C : (e + 1) * C], acc[:])
+        banks = [late_psum.tile([P, 4 * C], F32, name="late_acc%d" % i) for i in range(2)]
+        last_acc = psum.tile([P, C], F32, name="y_acc")
+        place = {e: banks[(e - 9) // 4][:, (e - 9) % 4 * C : ((e - 9) % 4 + 1) * C] for e in range(9, 17)}
+        place[17] = last_acc[:]
+        for group in late_groups:
+            second_product(*group, [place[e] for e in group[0]])
+            if group[0][0] in (11, 15):
+                first = group[0][0] - 2
+                nc.scalar.copy(y[:, first * C : (first + 4) * C], banks[(first - 9) // 4][:])
+        nc.vector.tensor_copy(y[:, 17 * C :], last_acc[:])
 
         for c, (t0, t1) in enumerate(TOKEN_CHUNKS):
             width = t1 - t0

@@ -23,13 +23,13 @@ PACK = 4
 LIST_ROWS = 16
 GATHER_EXPERTS = 3
 LATE_FROM = 9
-LAST_SPLIT = 48
+LAST_SPLIT = 44
 SINGLES_FROM = 0
-EARLY_W2 = {0: (0,), 1: (1, 2, 3, 4), 5: (5, 6, 7, 8)}
+EARLY_W2 = {0: (0, 1, 2, 3), 4: (4, 5, 6, 7, 8)}
 STREAM_BUFS = 12
 H_AT = 256
 W2_AT = 1024
-TOKEN_CHUNKS = ((0, 576), (576, 768))
+TOKEN_CHUNKS = ((0, 384), (384, 768))
 
 
 def tile_moe_pkd_glu_silu_kernel(
@@ -46,7 +46,7 @@ def tile_moe_pkd_glu_silu_kernel(
         y = keep.tile([P, S], F32, name="y")
 
         first_stage = [keep.tile([P, H * PACK], BF16, name="stage1_%d" % i, align_bytes=64) for i in range(2)]
-        third_stage = [keep.tile([P, H * PACK], BF16, name="stage3_%d" % i, align_bytes=64) for i in range(1)]
+        third_stage = keep.tile([P, H * PACK], BF16, name="stage3", align_bytes=64)
         late_stage = [keep.tile([P, H * PACK], BF16, name="late_stage%d" % i, align_bytes=64) for i in range(2)]
 
         def load(weights, experts, pool=stream, name="raw"):
@@ -92,23 +92,26 @@ def tile_moe_pkd_glu_silu_kernel(
                 )
             return acc
 
-        def hidden(e, tokens):
+        def gate_branch(e, tokens):
             stage = first_stage[e % 2]
             round_first(raw1[e], stage[:], [(nc.vector.tensor_copy, 0, P)])
             a = first_product(quantize(work, stage[:], H, "w1"), tokens, e, "a")
-            if e < E - 1:
+            silu_a = work.tile([P, C, PACK], F32, name="silu_a")
+            nc.scalar.activation(silu_a[:], a[:].rearrange("p t c -> p c t"), SILU)
+            return silu_a
+
+        def linear_branch(e, tokens):
+            if e < E - 2:
                 shares = [(nc.scalar.copy, 0, P)]
             else:
                 shares = [(nc.scalar.copy, 0, LAST_SPLIT), (nc.vector.tensor_copy, LAST_SPLIT, P)]
-            round_first(raw3[e], third_stage[0][:], shares)
-            b = first_product(quantize(work, third_stage[0][:], H, "w3"), tokens, e, "b")
-            silu_a = work.tile([P, C, PACK], F32, name="silu_a", bufs=2)
-            nc.scalar.activation(silu_a[:], a[:].rearrange("p t c -> p c t"), SILU)
-            h = stage[:, H_AT : H_AT + C * PACK]
+            round_first(raw3[e], third_stage[:], shares)
+            return first_product(quantize(work, third_stage[:], H, "w3"), tokens, e, "b")
+
+        def multiply(h, b, silu_a):
             nc.vector.tensor_tensor(
                 h.rearrange("p (c t) -> p c t", t=PACK), b[:].rearrange("p t c -> p c t"), silu_a[:], MULT
             )
-            return quantize(keep, h, C, "h%d" % e)
 
         def second_product(experts, copies, stage, at, places):
             count = len(experts)
@@ -124,18 +127,18 @@ def tile_moe_pkd_glu_silu_kernel(
                     out=places[g],
                     lhsT=codes[:, g * N : (g + 1) * N].bitcast(FP8X4),
                     lhsT_scale=scales[:, g * N : (g + 1) * N],
-                    rhs=h_mx[e][0][:].bitcast(FP8X4),
-                    rhs_scale=h_mx[e][1][:],
+                    rhs=h_mx[e][0].bitcast(FP8X4),
+                    rhs_scale=h_mx[e][1],
                     start=True,
                     stop=True,
                 )
 
         on_scalar, on_vector = nc.scalar.copy, nc.vector.tensor_copy
+        late_loads = ((9, 10), (11, 12), (13, 14), (15, 16), (17,))
         late_groups = [
-            ((9, 10), (on_vector, on_vector), late_stage[0], 0),
+            ((9, 10), (on_scalar, on_scalar), late_stage[0], 0),
             ((11, 12), (on_scalar, on_scalar), late_stage[0], 1024),
-            ((13, 14), (on_scalar, on_scalar), late_stage[1], 0),
-            ((15, 16), (on_vector, on_vector), late_stage[1], 1024),
+            ((13, 14, 15, 16), (on_scalar, on_scalar, on_vector, on_vector), late_stage[1], 0),
             ((17,), (on_scalar,), first_stage[0], 0),
         ]
         back_lists = []
@@ -152,52 +155,71 @@ def tile_moe_pkd_glu_silu_kernel(
                 token_scales[32 * q : 32 * q + 4, :],
                 x_scales[0, 4 * q : 4 * q + 4, :].bitcast(I32),
             )
-        for e in range(E):
-            if e not in raw1:
-                raw1.update(load(w1, (e, e + 1) if e < SINGLES_FROM - 1 else (e,)))
+        for e in range(E - 2):
+            if e > 0:
+                raw1.update(load(w1, (e,)))
             if e in EARLY_W2:
                 raw2.update(load(w2, EARLY_W2[e]))
-            if e not in raw3:
-                raw3.update(load(w3, (e, e + 1) if e < SINGLES_FROM - 1 else (e,)))
-            if e == 0:
-                for r, pos in enumerate((pos1, pos2, pos3)):
-                    back = keep.tile([P, T // LIST_ROWS], U16, name="back_list%d" % r)
-                    nc.sync.dma_start(back[:], pos)
-                    back_lists.append(back)
+            raw3.update(load(w3, (e,)))
             if e % GATHER_EXPERTS == 0:
                 tokens = gather_tokens(e // GATHER_EXPERTS)
-            if e == E - 1:
-                for group in late_groups:
-                    raw2.update(load(w2, group[0]))
-                gates = []
-                for t0, t1 in TOKEN_CHUNKS:
-                    chunk = stream.tile([P, TOP, t1 - t0], F32, name="gates", tag="raw")
-                    nc.sync.dma_start(chunk[:], gate[:, :, t0:t1].rearrange("r p t -> p r t"))
-                    gates.append(chunk)
-            h_mx[e] = hidden(e, tokens)
+            silu_a = gate_branch(e, tokens)
+            b = linear_branch(e, tokens)
+            h = first_stage[e % 2][:, H_AT : H_AT + C * PACK]
+            multiply(h, b, silu_a)
+            codes, scales = quantize(keep, h, C, "h%d" % e)
+            h_mx[e] = (codes[:], scales[:])
             if e < LATE_FROM:
                 acc = psum.tile([P, C], F32, name="y_acc")
                 second_product((e,), (on_scalar,), first_stage[e % 2], W2_AT, [acc[:]])
                 nc.scalar.copy(y[:, e * C : (e + 1) * C], acc[:])
-        banks = [late_psum.tile([P, 4 * C], F32, name="late_acc%d" % i) for i in range(2)]
-        last_acc = psum.tile([P, C], F32, name="y_acc")
-        place = {e: banks[(e - 9) // 4][:, (e - 9) % 4 * C : ((e - 9) % 4 + 1) * C] for e in range(9, 17)}
-        place[17] = last_acc[:]
+
+        last_two = (E - 2, E - 1)
+        for e in last_two:
+            raw1.update(load(w1, (e,)))
+        for e in last_two:
+            raw3.update(load(w3, (e,)))
+        for experts in late_loads:
+            raw2.update(load(w2, experts))
+        for r, pos in enumerate((pos1, pos2, pos3)):
+            back = keep.tile([P, T // LIST_ROWS], U16, name="back_list%d" % r)
+            nc.sync.dma_start(back[:], pos)
+            back_lists.append(back)
+        gates = []
+        for r0, r1 in ((0, 1), (1, TOP)):
+            rows = stream.tile([P, r1 - r0, T], F32, name="gates", tag="raw")
+            nc.sync.dma_start(rows[:], gate[r0:r1].rearrange("r p t -> p r t"))
+            gates.extend(rows[:, r] for r in range(r1 - r0))
+        silu_last = [gate_branch(e, tokens) for e in last_two]
+        b_last = [linear_branch(e, tokens) for e in last_two]
+        for g in range(2):
+            multiply(third_stage[:, g * C * PACK : (g + 1) * C * PACK], b_last[g], silu_last[g])
+        codes, scales = quantize(keep, third_stage[:, : 2 * C * PACK], 2 * C, "h_last")
+        for g, e in enumerate(last_two):
+            h_mx[e] = (codes[:, g * C : (g + 1) * C], scales[:, g * C : (g + 1) * C])
+
+        bank_of = ((9, 10, 11, 12), (13, 14, 15), (16, 17))
+        banks = [late_psum.tile([P, len(bank_of[i]) * C], F32, name="late_acc%d" % i) for i in range(2)]
+        banks.append(psum.tile([P, 2 * C], F32, name="y_acc"))
+        place = {e: banks[i][:, g * C : (g + 1) * C] for i in range(3) for g, e in enumerate(bank_of[i])}
         for group in late_groups:
             second_product(*group, [place[e] for e in group[0]])
-            if group[0][0] in (11, 15):
-                first = group[0][0] - 2
-                nc.scalar.copy(y[:, first * C : (first + 4) * C], banks[(first - 9) // 4][:])
-        nc.vector.tensor_copy(y[:, 17 * C :], last_acc[:])
+            if group[0][-1] == 12:
+                nc.scalar.copy(y[:, 9 * C : 13 * C], banks[0][:])
+            if group[0][-1] == 16:
+                nc.scalar.copy(y[:, 13 * C : 16 * C], banks[1][:])
+        nc.vector.tensor_copy(y[:, 16 * C :], banks[2][:])
 
+        parts = [keep.tile([P, T], F32, name="part%d" % r) for r in range(TOP)]
+        pair = keep.tile([P, T], F32, name="pair")
+        total = keep.tile([P, T], F32, name="total")
+        for r in range(TOP - 1):
+            nc.vector.tensor_tensor(parts[r][:], y[:].indirect(back_lists[r][:]), gates[r], MULT)
         for c, (t0, t1) in enumerate(TOKEN_CHUNKS):
-            width = t1 - t0
-            parts = [keep.tile([P, width], F32, name="part%d_%d" % (r, t0)) for r in range(TOP)]
-            pair = keep.tile([P, width], F32, name="pair%d" % t0)
-            total = keep.tile([P, width], F32, name="total%d" % t0)
-            for r in range(TOP):
-                offsets = back_lists[r][:, t0 // LIST_ROWS : t1 // LIST_ROWS]
-                nc.vector.tensor_tensor(parts[r][:], y[:].indirect(offsets), gates[c][:, r, :], MULT)
-            nc.vector.tensor_tensor(pair[:], parts[0][:], parts[1][:], ADD)
-            nc.vector.tensor_tensor(total[:], pair[:], parts[2][:], ADD)
-            nc.sync.dma_start(out[:, t0:t1], total[:])
+            offsets = back_lists[2][:, t0 // LIST_ROWS : t1 // LIST_ROWS]
+            nc.vector.tensor_tensor(parts[2][:, t0:t1], y[:].indirect(offsets), gates[2][:, t0:t1], MULT)
+            if c == 0:
+                nc.vector.tensor_tensor(pair[:], parts[0][:], parts[1][:], ADD)
+        for t0, t1 in TOKEN_CHUNKS:
+            nc.vector.tensor_tensor(total[:, t0:t1], pair[:, t0:t1], parts[2][:, t0:t1], ADD)
+            nc.sync.dma_start(out[:, t0:t1], total[:, t0:t1])

@@ -22,10 +22,11 @@ P = 128
 PACK = 4
 LIST_ROWS = 16
 GATHER_EXPERTS = 3
-LATE_FROM = 9
+LATE_FROM = 7
+FIRST_SPLIT = 16
 LAST_SPLIT = 44
 SINGLES_FROM = 0
-EARLY_W2 = {0: (0, 1, 2, 3), 4: (4, 5, 6, 7, 8)}
+EARLY_W2 = {0: (0, 1, 2, 3), 4: (4, 5, 6)}
 STREAM_BUFS = 12
 H_AT = 256
 W2_AT = 1024
@@ -59,8 +60,8 @@ def tile_moe_pkd_glu_silu_kernel(
         def gather_tokens(g):
             width = GATHER_EXPERTS * C
             offsets = slot_list[:, g * width // LIST_ROWS : (g + 1) * width // LIST_ROWS]
-            words = work.tile([P, width], U32, name="slot_words", align_bytes=64)
-            scales = work.tile([P, width], U8, name="slot_scales", align_bytes=64)
+            words = work.tile([P, width], U32, name="slot_words", align_bytes=64, bufs=4)
+            scales = work.tile([P, width], U8, name="slot_scales", align_bytes=64, bufs=4)
             nc.vector.tensor_copy(words[:], token_words[:].bitcast(U32).indirect(offsets))
             nc.vector.tensor_copy(scales[:], token_scales[:].bitcast(U8).indirect(offsets))
             return words, scales
@@ -94,7 +95,11 @@ def tile_moe_pkd_glu_silu_kernel(
 
         def gate_branch(e, tokens):
             stage = first_stage[e % 2]
-            round_first(raw1[e], stage[:], [(nc.vector.tensor_copy, 0, P)])
+            if e < LATE_FROM:
+                shares = [(nc.vector.tensor_copy, 0, P)]
+            else:
+                shares = [(nc.scalar.copy, 0, FIRST_SPLIT), (nc.vector.tensor_copy, FIRST_SPLIT, P)]
+            round_first(raw1[e], stage[:], shares)
             a = first_product(quantize(work, stage[:], H, "w1"), tokens, e, "a")
             silu_a = work.tile([P, C, PACK], F32, name="silu_a")
             nc.scalar.activation(silu_a[:], a[:].rearrange("p t c -> p c t"), SILU)
@@ -134,12 +139,12 @@ def tile_moe_pkd_glu_silu_kernel(
                 )
 
         on_scalar, on_vector = nc.scalar.copy, nc.vector.tensor_copy
-        late_loads = ((9, 10), (11, 12), (13, 14), (15, 16), (17,))
+        late_loads = ((7, 8), (9, 10), (11, 12), (13, 14), (15, 16), (17,))
         late_groups = [
-            ((9, 10), (on_scalar, on_scalar), late_stage[0], 0),
-            ((11, 12), (on_scalar, on_scalar), late_stage[0], 1024),
-            ((13, 14, 15, 16), (on_scalar, on_scalar, on_vector, on_vector), late_stage[1], 0),
-            ((17,), (on_scalar,), first_stage[0], 0),
+            ((7, 8, 9, 10), (on_scalar,) * 4, late_stage[0], 0),
+            ((11, 12, 13, 14), (on_scalar, on_vector) * 2, late_stage[1], 0),
+            ((15, 16), (on_scalar, on_vector), first_stage[0], 0),
+            ((17,), (on_vector,), first_stage[0], 1024),
         ]
         back_lists = []
         raw1, raw3, raw2, h_mx = {}, {}, {}, {}
@@ -198,17 +203,17 @@ def tile_moe_pkd_glu_silu_kernel(
         for g, e in enumerate(last_two):
             h_mx[e] = (codes[:, g * C : (g + 1) * C], scales[:, g * C : (g + 1) * C])
 
-        bank_of = ((9, 10, 11, 12), (13, 14, 15), (16, 17))
-        banks = [late_psum.tile([P, len(bank_of[i]) * C], F32, name="late_acc%d" % i) for i in range(2)]
-        banks.append(psum.tile([P, 2 * C], F32, name="y_acc"))
-        place = {e: banks[i][:, g * C : (g + 1) * C] for i in range(3) for g, e in enumerate(bank_of[i])}
+        bank_of = ((7, 9, 11, 13), (8, 10, 12, 14), (15, 16, 17))
+        banks = [late_psum.tile([P, 4, C], F32, name="late_acc%d" % i) for i in range(2)]
+        banks.append(psum.tile([P, 3, C], F32, name="y_acc"))
+        place = {e: banks[i][:, g, :] for i in range(3) for g, e in enumerate(bank_of[i])}
+        by_expert = y[:].rearrange("p (e c) -> p e c", c=C)
         for group in late_groups:
             second_product(*group, [place[e] for e in group[0]])
-            if group[0][-1] == 12:
-                nc.scalar.copy(y[:, 9 * C : 13 * C], banks[0][:])
-            if group[0][-1] == 16:
-                nc.scalar.copy(y[:, 13 * C : 16 * C], banks[1][:])
-        nc.vector.tensor_copy(y[:, 16 * C :], banks[2][:])
+            if group[0][-1] == 14:
+                nc.scalar.copy(by_expert[:, 7:15:2, :], banks[0][:])
+                nc.scalar.copy(by_expert[:, 8:15:2, :], banks[1][:])
+        nc.vector.tensor_copy(by_expert[:, 15:, :], banks[2][:])
 
         parts = [keep.tile([P, T], F32, name="part%d" % r) for r in range(TOP)]
         pair = keep.tile([P, T], F32, name="pair")

@@ -1,6 +1,7 @@
 from contextlib import ExitStack
 
 import concourse.mybir as mybir
+from concourse.masks import make_identity
 
 K, T, E, C, H, N = 512, 768, 18, 128, 512, 128
 TOP = 3
@@ -22,15 +23,15 @@ P = 128
 PACK = 4
 LIST_ROWS = 16
 GATHER_EXPERTS = 3
-LATE_FROM = 7
-FIRST_SPLIT = 16
-LAST_SPLIT = 44
-SINGLES_FROM = 0
-EARLY_W2 = {0: (0, 1, 2, 3), 4: (4, 5, 6)}
-STREAM_BUFS = 12
-H_AT = 256
-W2_AT = 1024
-TOKEN_CHUNKS = ((0, 384), (384, 768))
+GATHER_BUFS = 3
+W1_SHARE = {17: 40}
+W3_SHARE = {16: 88, 17: 40}
+EARLY_W2 = {0: (0, 1, 2, 3), 3: (4, 5, 6, 7), 7: (8, 9, 10, 11)}
+BETWEEN = (12, 13)
+LATE_LOADS = ((16, 17), (14, 15))
+LATE_W2 = tuple(range(12, 18))
+STREAM_BUFS = 14
+TURNED_BLOCKS = 3
 
 
 def tile_moe_pkd_glu_silu_kernel(
@@ -40,45 +41,48 @@ def tile_moe_pkd_glu_silu_kernel(
     with ExitStack() as ctx:
         keep = ctx.enter_context(tc.tile_pool(name="keep", bufs=1))
         stream = ctx.enter_context(tc.tile_pool(name="stream", bufs=STREAM_BUFS))
-        work = ctx.enter_context(tc.tile_pool(name="work", bufs=3))
+        work = ctx.enter_context(tc.tile_pool(name="work", bufs=2))
         psum = ctx.enter_context(tc.psum_pool(name="psum", bufs=2))
-        late_psum = ctx.enter_context(tc.psum_pool(name="late_psum", bufs=1))
 
         y = keep.tile([P, S], F32, name="y")
+        identity = keep.tile([P, P], F32, name="identity")
+        make_identity(nc, identity[:])
+        on_scalar, on_vector = nc.scalar.copy, nc.vector.tensor_copy
 
-        first_stage = [keep.tile([P, H * PACK], BF16, name="stage1_%d" % i, align_bytes=64) for i in range(2)]
-        third_stage = keep.tile([P, H * PACK], BF16, name="stage3", align_bytes=64)
-        late_stage = [keep.tile([P, H * PACK], BF16, name="late_stage%d" % i, align_bytes=64) for i in range(2)]
-
-        def load(weights, experts, pool=stream, name="raw"):
-            raw = pool.tile([P, len(experts), PACK, weights.shape[2]], F32, name=name)
+        def load(weights, experts):
+            raw = stream.tile([P, len(experts), PACK, weights.shape[2]], F32, name="raw", align_bytes=64)
             nc.sync.dma_start(
                 raw[:], weights[experts[0] : experts[-1] + 1].rearrange("g (p j) c -> p g j c", j=PACK)
             )
-            return {e: raw[:, g] for g, e in enumerate(experts)}
+            return raw
 
         def gather_tokens(g):
             width = GATHER_EXPERTS * C
             offsets = slot_list[:, g * width // LIST_ROWS : (g + 1) * width // LIST_ROWS]
-            words = work.tile([P, width], U32, name="slot_words", align_bytes=64, bufs=4)
-            scales = work.tile([P, width], U8, name="slot_scales", align_bytes=64, bufs=4)
+            words = work.tile([P, width], U32, name="slot_words", align_bytes=64, bufs=GATHER_BUFS)
+            scales = work.tile([P, width], U8, name="slot_scales", align_bytes=64, bufs=GATHER_BUFS)
             nc.vector.tensor_copy(words[:], token_words[:].bitcast(U32).indirect(offsets))
             nc.vector.tensor_copy(scales[:], token_scales[:].bitcast(U8).indirect(offsets))
             return words, scales
 
-        def quantize(pool, rounded, width, name):
-            codes = pool.tile([P, width], U32, name=name + "_codes", align_bytes=64)
-            scales = pool.tile([P, width], U8, name=name + "_scales", align_bytes=64)
+        def quantize(rounded, width, name, bufs=2):
+            codes = work.tile([P, width], U32, name=name + "_codes", align_bytes=64, bufs=bufs)
+            scales = work.tile([P, width], U8, name=name + "_scales", align_bytes=64, bufs=bufs)
             nc.vector.quantize_mx(out=codes[:].bitcast(FP8X4), scales=scales[:], in_=rounded)
             return codes, scales
 
-        def round_first(raw, rounded, shares):
-            dst = rounded.rearrange("p (t m j) -> p m j t", t=PACK, j=PACK)
-            src = raw.rearrange("p j (m t) -> p m j t", t=PACK)
-            for copy, m0, m1 in shares:
-                copy(dst[:, m0:m1], src[:, m0:m1])
+        def round_first(raw, name, share):
+            rounded = work.tile([P, H * PACK], BF16, name=name, align_bytes=64)
+            dst = rounded[:].rearrange("p (t m j) -> p m j t", t=PACK, j=PACK)
+            src = raw[:, 0].rearrange("p j (m t) -> p m j t", t=PACK)
+            if share > 0:
+                on_scalar(dst[:, :share], src[:, :share])
+            if share < P:
+                on_vector(dst[:, share:], src[:, share:])
+            return rounded
 
-        def first_product(weights, tokens, e, name):
+        def first_product(weights, e, name):
+            words, scales = tokens[e // GATHER_EXPERTS]
             cols = slice((e % GATHER_EXPERTS) * C, (e % GATHER_EXPERTS + 1) * C)
             acc = psum.tile([P, PACK, C], F32, name=name)
             for t in range(PACK):
@@ -86,145 +90,147 @@ def tile_moe_pkd_glu_silu_kernel(
                     out=acc[:, t, :],
                     lhsT=weights[0][:, t * P : (t + 1) * P].bitcast(FP8X4),
                     lhsT_scale=weights[1][:, t * P : (t + 1) * P],
-                    rhs=tokens[0][:, cols].bitcast(FP8X4),
-                    rhs_scale=tokens[1][:, cols],
+                    rhs=words[:, cols].bitcast(FP8X4),
+                    rhs_scale=scales[:, cols],
                     start=True,
                     stop=True,
                 )
             return acc
 
-        def gate_branch(e, tokens):
-            stage = first_stage[e % 2]
-            if e < LATE_FROM:
-                shares = [(nc.vector.tensor_copy, 0, P)]
-            else:
-                shares = [(nc.scalar.copy, 0, FIRST_SPLIT), (nc.vector.tensor_copy, FIRST_SPLIT, P)]
-            round_first(raw1[e], stage[:], shares)
-            a = first_product(quantize(work, stage[:], H, "w1"), tokens, e, "a")
-            silu_a = work.tile([P, C, PACK], F32, name="silu_a")
-            nc.scalar.activation(silu_a[:], a[:].rearrange("p t c -> p c t"), SILU)
-            return silu_a
-
-        def linear_branch(e, tokens):
-            if e < E - 2:
-                shares = [(nc.scalar.copy, 0, P)]
-            else:
-                shares = [(nc.scalar.copy, 0, LAST_SPLIT), (nc.vector.tensor_copy, LAST_SPLIT, P)]
-            round_first(raw3[e], third_stage[:], shares)
-            return first_product(quantize(work, third_stage[:], H, "w3"), tokens, e, "b")
-
-        def multiply(h, b, silu_a):
+        def multiply(e, h):
             nc.vector.tensor_tensor(
-                h.rearrange("p (c t) -> p c t", t=PACK), b[:].rearrange("p t c -> p c t"), silu_a[:], MULT
+                h.rearrange("p (q c t) -> p q c t", q=PACK, t=PACK),
+                b[e][:].rearrange("p t (q c) -> p q c t", q=PACK),
+                silu_a[e],
+                MULT,
             )
 
-        def second_product(experts, copies, stage, at, places):
+        def round_w2(experts, raw, copy, name, bufs):
             count = len(experts)
-            rounded2 = stage[:, at : at + count * N * PACK]
-            for g, e in enumerate(experts):
-                copies[g](
-                    rounded2[:, g * N * PACK : (g + 1) * N * PACK].rearrange("p (m i j) -> p m j i", i=PACK, j=PACK),
-                    raw2[e].rearrange("p j (m i) -> p m j i", i=PACK),
-                )
-            codes, scales = quantize(work, rounded2, count * N, "w2")
-            for g, e in enumerate(experts):
-                nc.tensor.matmul_mx(
-                    out=places[g],
-                    lhsT=codes[:, g * N : (g + 1) * N].bitcast(FP8X4),
-                    lhsT_scale=scales[:, g * N : (g + 1) * N],
-                    rhs=h_mx[e][0].bitcast(FP8X4),
-                    rhs_scale=h_mx[e][1],
-                    start=True,
-                    stop=True,
-                )
+            rounded = work.tile([P, count * N * PACK], BF16, name=name, align_bytes=64, bufs=bufs)
+            copy(
+                rounded[:].rearrange("p (m i j) -> p m j i", i=PACK, j=PACK).rearrange("p (g m) j i -> p g m j i", g=count),
+                raw[:].rearrange("p g j (m i) -> p g m j i", i=PACK),
+            )
+            return rounded
 
-        on_scalar, on_vector = nc.scalar.copy, nc.vector.tensor_copy
-        late_loads = ((7, 8), (9, 10), (11, 12), (13, 14), (15, 16), (17,))
-        late_groups = [
-            ((7, 8, 9, 10), (on_scalar,) * 4, late_stage[0], 0),
-            ((11, 12, 13, 14), (on_scalar, on_vector) * 2, late_stage[1], 0),
-            ((15, 16), (on_scalar, on_vector), first_stage[0], 0),
-            ((17,), (on_vector,), first_stage[0], 1024),
-        ]
-        back_lists = []
-        raw1, raw3, raw2, h_mx = {}, {}, {}, {}
-        raw1.update(load(w1, (0,)))
+        def quantize_w2(experts, rounded, name, bufs):
+            count = len(experts)
+            codes, scales = quantize(rounded[:], count * N, name, bufs)
+            for g, e in enumerate(experts):
+                w2_mx[e] = (codes[:, g * N : (g + 1) * N], scales[:, g * N : (g + 1) * N])
+
+        def second_product(e, place):
+            nc.tensor.matmul_mx(
+                out=place,
+                lhsT=w2_mx[e][0].bitcast(FP8X4),
+                lhsT_scale=w2_mx[e][1],
+                rhs=h_mx[e][0][:].bitcast(FP8X4),
+                rhs_scale=h_mx[e][1][:],
+                start=True,
+                stop=True,
+            )
+
+        tokens, b, silu_a, h_mx, w2_mx = {}, {}, {}, {}, {}
+        raw1 = load(w1, (0,))
         slot_list = keep.tile([P, S // LIST_ROWS], U16, name="slot_list")
         nc.sync.dma_start(slot_list[:], offs)
         token_words = keep.tile([P, T], I32, name="token_words")
         nc.sync.dma_start(token_words[:], x_words[0].rearrange("p t r -> p (t r)").bitcast(I32))
         token_scales = keep.tile([P, T // 4], I32, name="token_scales")
+        loaded_scales = keep.tile([P, T // 4], I32, name="loaded_scales")
         nc.vector.memset(token_scales[:], 0)
         for q in range(4):
-            nc.sync.dma_start(
-                token_scales[32 * q : 32 * q + 4, :],
-                x_scales[0, 4 * q : 4 * q + 4, :].bitcast(I32),
-            )
-        for e in range(E - 2):
+            rows = slice(32 * q, 32 * q + 4)
+            nc.sync.dma_start(loaded_scales[rows, :], x_scales[0, 4 * q : 4 * q + 4, :].bitcast(I32))
+            nc.vector.tensor_copy(token_scales[rows, :], loaded_scales[rows, :])
+        for e in range(E):
             if e > 0:
-                raw1.update(load(w1, (e,)))
+                raw1 = load(w1, (e,))
+            if e == E - 1:
+                raw_between = load(w2, BETWEEN)
+            raw3 = load(w3, (e,))
             if e in EARLY_W2:
-                raw2.update(load(w2, EARLY_W2[e]))
-            raw3.update(load(w3, (e,)))
+                raw2 = load(w2, EARLY_W2[e])
             if e % GATHER_EXPERTS == 0:
-                tokens = gather_tokens(e // GATHER_EXPERTS)
-            silu_a = gate_branch(e, tokens)
-            b = linear_branch(e, tokens)
-            h = first_stage[e % 2][:, H_AT : H_AT + C * PACK]
-            multiply(h, b, silu_a)
-            codes, scales = quantize(keep, h, C, "h%d" % e)
-            h_mx[e] = (codes[:], scales[:])
-            if e < LATE_FROM:
-                acc = psum.tile([P, C], F32, name="y_acc")
-                second_product((e,), (on_scalar,), first_stage[e % 2], W2_AT, [acc[:]])
-                nc.scalar.copy(y[:, e * C : (e + 1) * C], acc[:])
+                tokens[e // GATHER_EXPERTS] = gather_tokens(e // GATHER_EXPERTS)
+            rounded1 = round_first(raw1, "rounded1", W1_SHARE.get(e, 0))
+            if e > 0:
+                h = raw1[:, 0, 0, : C * PACK // 2].bitcast(BF16)
+                multiply(e - 1, h)
+            a = first_product(quantize(rounded1[:], H, "w1"), e, "a")
+            if e > 0:
+                h_mx[e - 1] = quantize(h, C, "h", bufs=len(LATE_W2) + 2)
+                if e - 1 not in LATE_W2:
+                    group = [x for x in EARLY_W2.values() if e - 1 in x][0]
+                    if e - 1 == group[0]:
+                        acc = psum.tile([P, len(group), C], F32, name="y_acc")
+                    second_product(e - 1, acc[:, e - 1 - group[0], :])
+                    if e - 1 == group[-1]:
+                        on_scalar(y[:, group[0] * C : e * C], acc[:].rearrange("p g c -> p (g c)"))
+            if e - 1 in EARLY_W2 and e > 1:
+                quantize_w2(EARLY_W2[e - 1], rounded2, "w2", 1)
+            if e == E - 1:
+                quantize_w2(BETWEEN, round_w2(BETWEEN, raw_between, on_scalar, "late_w2", 3), "late_w2", 3)
+            rounded3 = round_first(raw3, "rounded3", W3_SHARE.get(e, P))
+            silu_a[e] = raw3[:, 0, :, :C].rearrange("p q (c t) -> p q c t", t=PACK)
+            nc.scalar.activation(silu_a[e], a[:].rearrange("p t (q c) -> p q c t", q=PACK), SILU)
+            b[e] = first_product(quantize(rounded3[:], H, "w3"), e, "b")
+            if e in EARLY_W2:
+                rounded2 = round_w2(EARLY_W2[e], raw2, on_scalar, "w2", 1)
+                if e == 0:
+                    quantize_w2(EARLY_W2[e], rounded2, "w2", 1)
 
-        last_two = (E - 2, E - 1)
-        for e in last_two:
-            raw1.update(load(w1, (e,)))
-        for e in last_two:
-            raw3.update(load(w3, (e,)))
-        for experts in late_loads:
-            raw2.update(load(w2, experts))
+        late_raw = {group: load(w2, group) for group in LATE_LOADS}
+        back_lists = []
         for r, pos in enumerate((pos1, pos2, pos3)):
             back = keep.tile([P, T // LIST_ROWS], U16, name="back_list%d" % r)
             nc.sync.dma_start(back[:], pos)
             back_lists.append(back)
-        gates = []
-        for r0, r1 in ((0, 1), (1, TOP)):
-            rows = stream.tile([P, r1 - r0, T], F32, name="gates", tag="raw")
-            nc.sync.dma_start(rows[:], gate[r0:r1].rearrange("r p t -> p r t"))
-            gates.extend(rows[:, r] for r in range(r1 - r0))
-        silu_last = [gate_branch(e, tokens) for e in last_two]
-        b_last = [linear_branch(e, tokens) for e in last_two]
-        for g in range(2):
-            multiply(third_stage[:, g * C * PACK : (g + 1) * C * PACK], b_last[g], silu_last[g])
-        codes, scales = quantize(keep, third_stage[:, : 2 * C * PACK], 2 * C, "h_last")
-        for g, e in enumerate(last_two):
-            h_mx[e] = (codes[:, g * C : (g + 1) * C], scales[:, g * C : (g + 1) * C])
+        split = TURNED_BLOCKS * P
+        gates = {}
+        for t0, t1 in ((0, split), (split, T)):
+            gates[t0] = stream.tile([P, TOP, t1 - t0], F32, name="gates", tag="raw", align_bytes=64)
+            nc.sync.dma_start(gates[t0][:], gate[:, :, t0:t1].rearrange("r p t -> p r t"))
 
-        bank_of = ((7, 9, 11, 13), (8, 10, 12, 14), (15, 16, 17))
-        banks = [late_psum.tile([P, 4, C], F32, name="late_acc%d" % i) for i in range(2)]
-        banks.append(psum.tile([P, 3, C], F32, name="y_acc"))
-        place = {e: banks[i][:, g, :] for i in range(3) for g, e in enumerate(bank_of[i])}
+        last_h = keep.tile([P, C * PACK], BF16, name="last_h", align_bytes=64)
+        multiply(E - 1, last_h[:])
+        h_mx[E - 1] = quantize(last_h[:], C, "h", bufs=len(LATE_W2) + 2)
+        for group in LATE_LOADS:
+            quantize_w2(group, round_w2(group, late_raw[group], on_scalar, "late_w2", 3), "late_w2", 3)
         by_expert = y[:].rearrange("p (e c) -> p e c", c=C)
-        for group in late_groups:
-            second_product(*group, [place[e] for e in group[0]])
-            if group[0][-1] == 14:
-                nc.scalar.copy(by_expert[:, 7:15:2, :], banks[0][:])
-                nc.scalar.copy(by_expert[:, 8:15:2, :], banks[1][:])
-        nc.vector.tensor_copy(by_expert[:, 15:, :], banks[2][:])
+        for first, copy in ((LATE_W2[1], on_vector), (LATE_W2[0], on_scalar)):
+            acc = psum.tile([P, len(LATE_W2) // 2, C], F32, name="y_acc")
+            for g, e in enumerate(range(first, E, 2)):
+                second_product(e, acc[:, g, :])
+            copy(by_expert[:, first::2, :], acc[:])
 
-        parts = [keep.tile([P, T], F32, name="part%d" % r) for r in range(TOP)]
-        pair = keep.tile([P, T], F32, name="pair")
-        total = keep.tile([P, T], F32, name="total")
-        for r in range(TOP - 1):
-            nc.vector.tensor_tensor(parts[r][:], y[:].indirect(back_lists[r][:]), gates[r], MULT)
-        for c, (t0, t1) in enumerate(TOKEN_CHUNKS):
-            offsets = back_lists[2][:, t0 // LIST_ROWS : t1 // LIST_ROWS]
-            nc.vector.tensor_tensor(parts[2][:, t0:t1], y[:].indirect(offsets), gates[2][:, t0:t1], MULT)
-            if c == 0:
-                nc.vector.tensor_tensor(pair[:], parts[0][:], parts[1][:], ADD)
-        for t0, t1 in TOKEN_CHUNKS:
-            nc.vector.tensor_tensor(total[:, t0:t1], pair[:, t0:t1], parts[2][:, t0:t1], ADD)
-            nc.sync.dma_start(out[:, t0:t1], total[:, t0:t1])
+        def gated(r, t0, t1):
+            part = keep.tile([P, t1 - t0], F32, name="part%d_%d" % (r, t0))
+            offsets = back_lists[r][:, t0 // LIST_ROWS : t1 // LIST_ROWS]
+            nc.vector.tensor_tensor(part[:], y[:].indirect(offsets), gates[t0][:, r], MULT)
+            return part
+
+        sums = [psum.tile([P, P], F32, name="sum%d" % k, tag="ab"[k % 2]) for k in range(TURNED_BLOCKS)]
+        for r in range(TOP):
+            part = gated(r, 0, split)
+            for k in range(TURNED_BLOCKS):
+                nc.tensor.matmul(
+                    sums[k][:], part[:, k * P : (k + 1) * P], identity[:],
+                    start=r == 0, stop=r == TOP - 1, is_transpose=True,
+                )
+        back_turned = psum.tile([P, TURNED_BLOCKS, P], F32, name="y_acc")
+        for k in range(TURNED_BLOCKS):
+            turned = keep.tile([P, P], F32, name="turned%d" % k)
+            on_scalar(turned[:], sums[k][:])
+            nc.tensor.transpose(back_turned[:, k, :], turned[:], identity[:])
+        head = keep.tile([P, split], F32, name="head")
+        on_scalar(head[:], back_turned[:].rearrange("p k c -> p (k c)"))
+        nc.sync.dma_start(out[:, :split], head[:])
+
+        parts = [gated(r, split, T) for r in range(TOP)]
+        pair = keep.tile([P, T - split], F32, name="pair")
+        rest = keep.tile([P, T - split], F32, name="rest")
+        nc.vector.tensor_tensor(pair[:], parts[0][:], parts[1][:], ADD)
+        nc.vector.tensor_tensor(rest[:], pair[:], parts[2][:], ADD)
+        nc.sync.dma_start(out[:, split:], rest[:])

@@ -73,8 +73,8 @@ def tile_moe_pkd_glu_silu_kernel(
 
         def round_first(raw, name, share):
             rounded = work.tile([P, H * PACK], BF16, name=name, align_bytes=64)
-            dst = rounded[:].rearrange("p (t m j) -> p m j t", t=PACK, j=PACK)
-            src = raw[:, 0].rearrange("p j (m t) -> p m j t", t=PACK)
+            dst = rounded[:].rearrange("p (t m u v) -> p m u t v", t=PACK, u=2, v=2)
+            src = raw[:, 0].rearrange("p (u v) (m t) -> p m u t v", t=PACK, u=2)
             if share > 0:
                 on_scalar(dst[:, :share], src[:, :share])
             if share < P:
@@ -108,10 +108,13 @@ def tile_moe_pkd_glu_silu_kernel(
         def round_w2(experts, raw, copy, name, bufs):
             count = len(experts)
             rounded = work.tile([P, count * N * PACK], BF16, name=name, align_bytes=64, bufs=bufs)
-            copy(
-                rounded[:].rearrange("p (m i j) -> p m j i", i=PACK, j=PACK).rearrange("p (g m) j i -> p g m j i", g=count),
-                raw[:].rearrange("p g j (m i) -> p g m j i", i=PACK),
-            )
+            for g in range(count):
+                copy(
+                    rounded[:, g * N * PACK : (g + 1) * N * PACK].rearrange(
+                        "p (m i u v) -> p m u i v", i=PACK, u=2, v=2
+                    ),
+                    raw[:, g].rearrange("p (u v) (m i) -> p m u i v", i=PACK, u=2),
+                )
             return rounded
 
         def quantize_w2(experts, rounded, name, bufs):

@@ -65,10 +65,16 @@ def tile_moe_pkd_glu_silu_kernel(
             nc.vector.tensor_copy(scales[:], token_scales[:].bitcast(U8).indirect(offsets))
             return words, scales
 
-        def quantize(rounded, width, name, bufs=2):
+        def quantize(rounded, width, name, bufs=2, pieces=1):
             codes = work.tile([P, width], U32, name=name + "_codes", align_bytes=64, bufs=bufs)
             scales = work.tile([P, width], U8, name=name + "_scales", align_bytes=64, bufs=bufs)
-            nc.vector.quantize_mx(out=codes[:].bitcast(FP8X4), scales=scales[:], in_=rounded)
+            step = width // pieces
+            for c in range(0, width, step):
+                nc.vector.quantize_mx(
+                    out=codes[:, c : c + step].bitcast(FP8X4),
+                    scales=scales[:, c : c + step],
+                    in_=rounded[:, c * PACK : (c + step) * PACK],
+                )
             return codes, scales
 
         def round_first(raw, name, share):
@@ -96,6 +102,21 @@ def tile_moe_pkd_glu_silu_kernel(
                     stop=True,
                 )
             return acc
+
+        def warm_up(weights, passes):
+            words, scales = tokens[(E - 1) // GATHER_EXPERTS]
+            for t in range(passes):
+                if t % 2 == 0:
+                    unread = psum.tile([P, 2, 2 * C], F32, name="unread")
+                nc.tensor.matmul_mx(
+                    out=unread[:, t % 2, :],
+                    lhsT=weights[0][:, t * P : (t + 1) * P].bitcast(FP8X4),
+                    lhsT_scale=weights[1][:, t * P : (t + 1) * P],
+                    rhs=words[:, : 2 * C].bitcast(FP8X4),
+                    rhs_scale=scales[:, : 2 * C],
+                    start=True,
+                    stop=True,
+                )
 
         def multiply(e, h):
             nc.vector.tensor_tensor(
@@ -161,7 +182,10 @@ def tile_moe_pkd_glu_silu_kernel(
             if e > 0:
                 h = raw1[:, 0, 0, : C * PACK // 2].bitcast(BF16)
                 multiply(e - 1, h)
-            a = first_product(quantize(rounded1[:], H, "w1"), e, "a")
+            w1_mx = quantize(rounded1[:], H, "w1")
+            a = first_product(w1_mx, e, "a")
+            if e == E - 1:
+                warm_up(w1_mx, 4)
             if e > 0:
                 h_mx[e - 1] = quantize(h, C, "h", bufs=len(LATE_W2) + 2)
                 if e - 1 not in LATE_W2:
@@ -178,7 +202,10 @@ def tile_moe_pkd_glu_silu_kernel(
             rounded3 = round_first(raw3, "rounded3", W3_SHARE.get(e, P))
             silu_a[e] = raw3[:, 0, :, :C].rearrange("p q (c t) -> p q c t", t=PACK)
             nc.scalar.activation(silu_a[e], a[:].rearrange("p t (q c) -> p q c t", q=PACK), SILU)
-            b[e] = first_product(quantize(rounded3[:], H, "w3"), e, "b")
+            w3_mx = quantize(rounded3[:], H, "w3", pieces=2 if e == E - 1 else 1)
+            b[e] = first_product(w3_mx, e, "b")
+            if e == E - 1:
+                warm_up(w3_mx, 4)
             if e in EARLY_W2:
                 rounded2 = round_w2(EARLY_W2[e], raw2, on_scalar, "w2", 1)
                 if e == 0:

@@ -22,16 +22,20 @@ SILU = mybir.ActivationFunctionType.Silu
 P = 128
 PACK = 4
 LIST_ROWS = 16
+LAST = E - 1
 GATHER_EXPERTS = 3
 GATHER_BUFS = 3
-W1_SHARE = {17: 40}
-W3_SHARE = {16: 88, 17: 40}
+W1_SHARE = {LAST: 40}
+W3_SHARE = {LAST - 1: 88, LAST: C // PACK}
 EARLY_W2 = {0: (0, 1, 2, 3), 3: (4, 5, 6, 7), 7: (8, 9, 10, 11)}
 BETWEEN = (12, 13)
 LATE_LOADS = ((16, 17), (14, 15))
-LATE_W2 = tuple(range(12, 18))
+LATE_W2 = tuple(range(12, E))
+LATE_BUFS = 5
+H_BUFS = len(LATE_W2) + 2
 STREAM_BUFS = 14
-TURNED_BLOCKS = 3
+WARM_PASSES = 4
+RANGE = 256
 
 
 def tile_moe_pkd_glu_silu_kernel(
@@ -103,9 +107,9 @@ def tile_moe_pkd_glu_silu_kernel(
                 )
             return acc
 
-        def warm_up(weights, passes):
-            words, scales = tokens[(E - 1) // GATHER_EXPERTS]
-            for t in range(passes):
+        def warm_up(weights):
+            words, scales = tokens[LAST // GATHER_EXPERTS]
+            for t in range(WARM_PASSES):
                 if t % 2 == 0:
                     unread = psum.tile([P, 2, 2 * C], F32, name="unread")
                 nc.tensor.matmul_mx(
@@ -126,15 +130,15 @@ def tile_moe_pkd_glu_silu_kernel(
                 MULT,
             )
 
-        def round_w2(experts, raw, copy, name, bufs):
+        def round_w2(experts, raw, name, bufs):
             count = len(experts)
             rounded = work.tile([P, count * N * PACK], BF16, name=name, align_bytes=64, bufs=bufs)
             for g in range(count):
-                copy(
+                on_scalar(
                     rounded[:, g * N * PACK : (g + 1) * N * PACK].rearrange(
-                        "p (m i u v) -> p m u i v", i=PACK, u=2, v=2
+                        "p (m s u v) -> p m u s v", s=PACK, u=2, v=2
                     ),
-                    raw[:, g].rearrange("p (u v) (m i) -> p m u i v", i=PACK, u=2),
+                    raw[:, g].rearrange("p (u v) (m s) -> p m u s v", s=PACK, u=2),
                 )
             return rounded
 
@@ -164,14 +168,14 @@ def tile_moe_pkd_glu_silu_kernel(
         token_scales = keep.tile([P, T // 4], I32, name="token_scales")
         loaded_scales = keep.tile([P, T // 4], I32, name="loaded_scales")
         nc.vector.memset(token_scales[:], 0)
-        for q in range(4):
-            rows = slice(32 * q, 32 * q + 4)
-            nc.sync.dma_start(loaded_scales[rows, :], x_scales[0, 4 * q : 4 * q + 4, :].bitcast(I32))
+        for quadrant in range(4):
+            rows = slice(32 * quadrant, 32 * quadrant + 4)
+            nc.sync.dma_start(loaded_scales[rows, :], x_scales[0, 4 * quadrant : 4 * quadrant + 4, :].bitcast(I32))
             nc.vector.tensor_copy(token_scales[rows, :], loaded_scales[rows, :])
         for e in range(E):
             if e > 0:
                 raw1 = load(w1, (e,))
-            if e == E - 1:
+            if e == LAST:
                 raw_between = load(w2, BETWEEN)
             raw3 = load(w3, (e,))
             if e in EARLY_W2:
@@ -184,30 +188,30 @@ def tile_moe_pkd_glu_silu_kernel(
                 multiply(e - 1, h)
             w1_mx = quantize(rounded1[:], H, "w1")
             a = first_product(w1_mx, e, "a")
-            if e == E - 1:
-                warm_up(w1_mx, 4)
+            if e == LAST:
+                warm_up(w1_mx)
             if e > 0:
-                h_mx[e - 1] = quantize(h, C, "h", bufs=len(LATE_W2) + 2)
+                h_mx[e - 1] = quantize(h, C, "h", bufs=H_BUFS)
                 if e - 1 not in LATE_W2:
                     group = [x for x in EARLY_W2.values() if e - 1 in x][0]
                     if e - 1 == group[0]:
-                        acc = psum.tile([P, len(group), C], F32, name="y_acc")
-                    second_product(e - 1, acc[:, e - 1 - group[0], :])
+                        group_acc = psum.tile([P, len(group), C], F32, name="y_acc")
+                    second_product(e - 1, group_acc[:, e - 1 - group[0], :])
                     if e - 1 == group[-1]:
-                        on_scalar(y[:, group[0] * C : e * C], acc[:].rearrange("p g c -> p (g c)"))
+                        on_scalar(y[:, group[0] * C : e * C], group_acc[:].rearrange("p g c -> p (g c)"))
             if e - 1 in EARLY_W2 and e > 1:
                 quantize_w2(EARLY_W2[e - 1], rounded2, "w2", 1)
-            if e == E - 1:
-                quantize_w2(BETWEEN, round_w2(BETWEEN, raw_between, on_scalar, "late_w2", 3), "late_w2", 3)
+            if e == LAST:
+                quantize_w2(BETWEEN, round_w2(BETWEEN, raw_between, "late_w2", LATE_BUFS), "late_w2", LATE_BUFS)
             rounded3 = round_first(raw3, "rounded3", W3_SHARE.get(e, P))
             silu_a[e] = raw3[:, 0, :, :C].rearrange("p q (c t) -> p q c t", t=PACK)
             nc.scalar.activation(silu_a[e], a[:].rearrange("p t (q c) -> p q c t", q=PACK), SILU)
-            w3_mx = quantize(rounded3[:], H, "w3", pieces=2 if e == E - 1 else 1)
+            w3_mx = quantize(rounded3[:], H, "w3", pieces=2 if e == LAST else 1)
             b[e] = first_product(w3_mx, e, "b")
-            if e == E - 1:
-                warm_up(w3_mx, 4)
+            if e == LAST:
+                warm_up(w3_mx)
             if e in EARLY_W2:
-                rounded2 = round_w2(EARLY_W2[e], raw2, on_scalar, "w2", 1)
+                rounded2 = round_w2(EARLY_W2[e], raw2, "w2", 1)
                 if e == 0:
                     quantize_w2(EARLY_W2[e], rounded2, "w2", 1)
 
@@ -217,50 +221,58 @@ def tile_moe_pkd_glu_silu_kernel(
             back = keep.tile([P, T // LIST_ROWS], U16, name="back_list%d" % r)
             nc.sync.dma_start(back[:], pos)
             back_lists.append(back)
-        split = TURNED_BLOCKS * P
         gates = {}
-        for t0, t1 in ((0, split), (split, T)):
-            gates[t0] = stream.tile([P, TOP, t1 - t0], F32, name="gates", tag="raw", align_bytes=64)
-            nc.sync.dma_start(gates[t0][:], gate[:, :, t0:t1].rearrange("r p t -> p r t"))
+        for t0 in range(0, T, RANGE):
+            gates[t0] = stream.tile([P, TOP, RANGE], F32, name="gates", tag="raw", align_bytes=64)
+            nc.sync.dma_start(gates[t0][:], gate[:, :, t0 : t0 + RANGE].rearrange("r p t -> p r t"))
 
         last_h = keep.tile([P, C * PACK], BF16, name="last_h", align_bytes=64)
-        multiply(E - 1, last_h[:])
-        h_mx[E - 1] = quantize(last_h[:], C, "h", bufs=len(LATE_W2) + 2)
+        multiply(LAST, last_h[:])
+        h_mx[LAST] = quantize(last_h[:], C, "h", bufs=H_BUFS)
         for group in LATE_LOADS:
-            quantize_w2(group, round_w2(group, late_raw[group], on_scalar, "late_w2", 3), "late_w2", 3)
+            for g, e in enumerate(group):
+                late_rounded = round_w2((e,), late_raw[group][:, g : g + 1], "late_w2", LATE_BUFS)
+                quantize_w2((e,), late_rounded, "late_w2", LATE_BUFS)
         by_expert = y[:].rearrange("p (e c) -> p e c", c=C)
-        for first, copy in ((LATE_W2[1], on_vector), (LATE_W2[0], on_scalar)):
-            acc = psum.tile([P, len(LATE_W2) // 2, C], F32, name="y_acc")
-            for g, e in enumerate(range(first, E, 2)):
-                second_product(e, acc[:, g, :])
-            copy(by_expert[:, first::2, :], acc[:])
+        for start, copy in ((LATE_W2[1], on_vector), (LATE_W2[0], on_scalar)):
+            late_acc = psum.tile([P, len(LATE_W2) // 2, C], F32, name="y_acc")
+            for g, e in enumerate(range(start, E, 2)):
+                second_product(e, late_acc[:, g, :])
+            copy(by_expert[:, start::2, :], late_acc[:])
 
-        def gated(r, t0, t1):
-            part = keep.tile([P, t1 - t0], F32, name="part%d_%d" % (r, t0))
-            offsets = back_lists[r][:, t0 // LIST_ROWS : t1 // LIST_ROWS]
-            nc.vector.tensor_tensor(part[:], y[:].indirect(offsets), gates[t0][:, r], MULT)
+        def gated(r, t0, lo, hi):
+            part = keep.tile([P, hi - lo], F32, name="part%d_%d" % (r, t0 + lo))
+            offsets = back_lists[r][:, (t0 + lo) // LIST_ROWS : (t0 + hi) // LIST_ROWS]
+            nc.vector.tensor_tensor(part[:], y[:].indirect(offsets), gates[t0][:, r, lo:hi], MULT)
             return part
 
-        sums = [psum.tile([P, P], F32, name="sum%d" % k, tag="ab"[k % 2]) for k in range(TURNED_BLOCKS)]
-        for r in range(TOP):
-            part = gated(r, 0, split)
-            for k in range(TURNED_BLOCKS):
-                nc.tensor.matmul(
-                    sums[k][:], part[:, k * P : (k + 1) * P], identity[:],
-                    start=r == 0, stop=r == TOP - 1, is_transpose=True,
-                )
-        back_turned = psum.tile([P, TURNED_BLOCKS, P], F32, name="y_acc")
-        for k in range(TURNED_BLOCKS):
-            turned = keep.tile([P, P], F32, name="turned%d" % k)
-            on_scalar(turned[:], sums[k][:])
-            nc.tensor.transpose(back_turned[:, k, :], turned[:], identity[:])
-        head = keep.tile([P, split], F32, name="head")
-        on_scalar(head[:], back_turned[:].rearrange("p k c -> p (k c)"))
-        nc.sync.dma_start(out[:, :split], head[:])
+        blocks = RANGE // P
+        for t0 in range(0, T - RANGE, RANGE):
+            sums = [psum.tile([P, P], F32, name="ab"[blk]) for blk in range(blocks)]
+            for r in range(TOP):
+                part = gated(r, t0, 0, RANGE)
+                for blk in range(blocks):
+                    nc.tensor.matmul(
+                        sums[blk][:], part[:, blk * P : (blk + 1) * P], identity[:],
+                        start=r == 0, stop=r == TOP - 1, is_transpose=True,
+                    )
+            back_turned = psum.tile([P, blocks, P], F32, name="y_acc")
+            for blk in range(blocks):
+                turned = keep.tile([P, P], F32, name="turned%d_%d" % (t0, blk))
+                on_scalar(turned[:], sums[blk][:])
+                nc.tensor.transpose(back_turned[:, blk, :], turned[:], identity[:])
+            head = keep.tile([P, RANGE], F32, name="head%d" % t0)
+            on_scalar(head[:], back_turned[:].rearrange("p blk c -> p (blk c)"))
+            nc.scalar.dma_start(out[:, t0 : t0 + RANGE], head[:])
 
-        parts = [gated(r, split, T) for r in range(TOP)]
-        pair = keep.tile([P, T - split], F32, name="pair")
-        rest = keep.tile([P, T - split], F32, name="rest")
-        nc.vector.tensor_tensor(pair[:], parts[0][:], parts[1][:], ADD)
-        nc.vector.tensor_tensor(rest[:], pair[:], parts[2][:], ADD)
-        nc.sync.dma_start(out[:, split:], rest[:])
+        t0 = T - RANGE
+        first, second = gated(0, t0, 0, RANGE), gated(1, t0, 0, RANGE)
+        third = [gated(2, t0, 0, P)]
+        pair = keep.tile([P, RANGE], F32, name="pair")
+        rest = keep.tile([P, RANGE], F32, name="rest")
+        nc.vector.tensor_tensor(pair[:], first[:], second[:], ADD)
+        third.append(gated(2, t0, P, RANGE))
+        for blk in range(blocks):
+            cols = slice(blk * P, (blk + 1) * P)
+            nc.vector.tensor_tensor(rest[:, cols], pair[:, cols], third[blk][:], ADD)
+        nc.sync.dma_start(out[:, t0:], rest[:])

@@ -18,6 +18,7 @@ FP8X4 = mybir.dt.float8_e4m3fn_x4
 MULT = mybir.AluOpType.mult
 ADD = mybir.AluOpType.add
 SILU = mybir.ActivationFunctionType.Silu
+COPY = mybir.ActivationFunctionType.Copy
 
 P = 128
 PACK = 4
@@ -240,39 +241,47 @@ def tile_moe_pkd_glu_silu_kernel(
                 second_product(e, late_acc[:, g, :])
             copy(by_expert[:, start::2, :], late_acc[:])
 
-        def gated(r, t0, lo, hi):
-            part = keep.tile([P, hi - lo], F32, name="part%d_%d" % (r, t0 + lo))
-            offsets = back_lists[r][:, (t0 + lo) // LIST_ROWS : (t0 + hi) // LIST_ROWS]
-            nc.vector.tensor_tensor(part[:], y[:].indirect(offsets), gates[t0][:, r, lo:hi], MULT)
-            return part
+        def offsets_of(r, lo, hi):
+            return back_lists[r][:, lo // LIST_ROWS : hi // LIST_ROWS]
+
+        early, middle, late = range(0, T, RANGE)
+        plain, parts = {}, {}
+        for r, t0 in ((2, early), (1, middle), (2, middle), (1, late), (2, late)):
+            plain[r, t0] = keep.tile([P, RANGE], F32, name="plain%d_%d" % (r, t0))
+            nc.scalar.activation(plain[r, t0][:], y[:].indirect(offsets_of(r, t0, t0 + RANGE)), COPY)
+        for t0, r in [(t0, r) for t0 in (early, middle, late) for r in range(TOP)]:
+            parts[r, t0] = keep.tile([P, RANGE], F32, name="part%d_%d" % (r, t0))
+            if (r, t0) in plain:
+                fetched = plain[r, t0][:]
+            else:
+                fetched = y[:].indirect(offsets_of(r, t0, t0 + RANGE))
+            nc.vector.tensor_tensor(parts[r, t0][:], fetched, gates[t0][:, r, :], MULT)
 
         blocks = RANGE // P
-        for t0 in range(0, T - RANGE, RANGE):
-            sums = [psum.tile([P, P], F32, name="ab"[blk]) for blk in range(blocks)]
+        sums, back_turned = {}, {}
+        for t0 in (early, middle):
+            sums[t0] = [psum.tile([P, P], F32, name="ab"[blk]) for blk in range(blocks)]
             for r in range(TOP):
-                part = gated(r, t0, 0, RANGE)
                 for blk in range(blocks):
                     nc.tensor.matmul(
-                        sums[blk][:], part[:, blk * P : (blk + 1) * P], identity[:],
+                        sums[t0][blk][:], parts[r, t0][:, blk * P : (blk + 1) * P], identity[:],
                         start=r == 0, stop=r == TOP - 1, is_transpose=True,
                     )
-            back_turned = psum.tile([P, blocks, P], F32, name="y_acc")
+        for t0 in (early, middle):
+            back_turned[t0] = psum.tile([P, blocks, P], F32, name="y_acc")
             for blk in range(blocks):
                 turned = keep.tile([P, P], F32, name="turned%d_%d" % (t0, blk))
-                on_scalar(turned[:], sums[blk][:])
-                nc.tensor.transpose(back_turned[:, blk, :], turned[:], identity[:])
+                on_scalar(turned[:], sums[t0][blk][:])
+                nc.tensor.transpose(back_turned[t0][:, blk, :], turned[:], identity[:])
+        for t0, queue in ((early, nc.sync), (middle, nc.scalar)):
             head = keep.tile([P, RANGE], F32, name="head%d" % t0)
-            on_scalar(head[:], back_turned[:].rearrange("p blk c -> p (blk c)"))
-            nc.scalar.dma_start(out[:, t0 : t0 + RANGE], head[:])
+            on_scalar(head[:], back_turned[t0][:].rearrange("p blk c -> p (blk c)"))
+            queue.dma_start(out[:, t0 : t0 + RANGE], head[:])
 
-        t0 = T - RANGE
-        first, second = gated(0, t0, 0, RANGE), gated(1, t0, 0, RANGE)
-        third = [gated(2, t0, 0, P)]
         pair = keep.tile([P, RANGE], F32, name="pair")
         rest = keep.tile([P, RANGE], F32, name="rest")
-        nc.vector.tensor_tensor(pair[:], first[:], second[:], ADD)
-        third.append(gated(2, t0, P, RANGE))
-        for blk in range(blocks):
-            cols = slice(blk * P, (blk + 1) * P)
-            nc.vector.tensor_tensor(rest[:, cols], pair[:, cols], third[blk][:], ADD)
-        nc.sync.dma_start(out[:, t0:], rest[:])
+        for total, first, second in ((pair, parts[0, late], parts[1, late]), (rest, pair, parts[2, late])):
+            for blk in range(blocks):
+                cols = slice(blk * P, (blk + 1) * P)
+                nc.vector.tensor_tensor(total[:, cols], first[:, cols], second[:, cols], ADD)
+        nc.sync.dma_start(out[:, late:], rest[:])

@@ -30,7 +30,7 @@ W1_SHARE = {LAST: 40}
 W3_SHARE = {LAST - 1: 88, LAST: C // PACK}
 EARLY_W2 = {0: (0, 1, 2, 3), 3: (4, 5, 6, 7), 7: (8, 9, 10, 11)}
 BETWEEN = (12, 13)
-LATE_LOADS = ((16, 17), (14, 15))
+LATE_LOADS = ((14, 15), (16, 17))
 LATE_W2 = tuple(range(12, E))
 LATE_BUFS = 5
 H_BUFS = len(LATE_W2) + 2
@@ -184,11 +184,11 @@ def tile_moe_pkd_glu_silu_kernel(
             if e % GATHER_EXPERTS == 0:
                 tokens[e // GATHER_EXPERTS] = gather_tokens(e // GATHER_EXPERTS)
             rounded1 = round_first(raw1, "rounded1", W1_SHARE.get(e, 0))
+            w1_mx = quantize(rounded1[:], H, "w1")
+            a = first_product(w1_mx, e, "a")
             if e > 0:
                 h = raw1[:, 0, 0, : C * PACK // 2].bitcast(BF16)
                 multiply(e - 1, h)
-            w1_mx = quantize(rounded1[:], H, "w1")
-            a = first_product(w1_mx, e, "a")
             if e == LAST:
                 warm_up(w1_mx)
             if e > 0:
@@ -227,19 +227,33 @@ def tile_moe_pkd_glu_silu_kernel(
             gates[t0] = stream.tile([P, TOP, RANGE], F32, name="gates", tag="raw", align_bytes=64)
             nc.sync.dma_start(gates[t0][:], gate[:, :, t0 : t0 + RANGE].rearrange("r p t -> p r t"))
 
-        last_h = keep.tile([P, C * PACK], BF16, name="last_h", align_bytes=64)
-        multiply(LAST, last_h[:])
-        h_mx[LAST] = quantize(last_h[:], C, "h", bufs=H_BUFS)
+        by_expert = y[:].rearrange("p (e c) -> p e c", c=C)
+
+        late = [e for group in LATE_LOADS for e in group]
+        late_rounded = {}
         for group in LATE_LOADS:
             for g, e in enumerate(group):
-                late_rounded = round_w2((e,), late_raw[group][:, g : g + 1], "late_w2", LATE_BUFS)
-                quantize_w2((e,), late_rounded, "late_w2", LATE_BUFS)
-        by_expert = y[:].rearrange("p (e c) -> p e c", c=C)
-        for start, copy in ((LATE_W2[1], on_vector), (LATE_W2[0], on_scalar)):
-            late_acc = psum.tile([P, len(LATE_W2) // 2, C], F32, name="y_acc")
-            for g, e in enumerate(range(start, E, 2)):
-                second_product(e, late_acc[:, g, :])
-            copy(by_expert[:, start::2, :], late_acc[:])
+                name, bufs = ("held", 1) if e == LAST - 1 else ("late_w2", LATE_BUFS)
+                late_rounded[e] = round_w2((e,), late_raw[group][:, g : g + 1], name, bufs)
+        quantize_w2(late[:1], late_rounded[late[0]], "late_w2", LATE_BUFS)
+        last_h = late_rounded[late[0]][:]
+        multiply(LAST, last_h)
+        for e in late[1:-1]:
+            quantize_w2((e,), late_rounded[e], "late_w2", LATE_BUFS)
+        last_codes = work.tile([P, C], U32, name="held", align_bytes=64, bufs=1)
+        last_scales = work.tile([P, C], U8, name="last_scales", align_bytes=64, bufs=1)
+        nc.vector.quantize_mx(out=last_codes[:].bitcast(FP8X4), scales=last_scales[:], in_=last_h)
+        h_mx[LAST] = (last_codes, last_scales)
+        quantize_w2((LAST,), late_rounded[LAST], "late_w2", LATE_BUFS)
+        inner = LATE_W2[1:-1]
+        outer_acc = psum.tile([P, 2, C], F32, name="y_acc")
+        inner_acc = psum.tile([P, len(inner), C], F32, name="y_acc")
+        second_product(LATE_W2[0], outer_acc[:, 0, :])
+        for g, e in enumerate(inner):
+            second_product(e, inner_acc[:, g, :])
+        second_product(LAST, outer_acc[:, 1, :])
+        on_scalar(by_expert[:, inner[0] : LAST, :], inner_acc[:])
+        on_vector(by_expert[:, LATE_W2[0] :: LAST - LATE_W2[0], :], outer_acc[:])
 
         def offsets_of(r, lo, hi):
             return back_lists[r][:, lo // LIST_ROWS : hi // LIST_ROWS]

@@ -37,6 +37,7 @@ H_BUFS = len(LATE_W2) + 2
 STREAM_BUFS = 14
 WARM_PASSES = 4
 RANGE = 256
+FUSED = (2, 1, 1)
 
 
 def tile_moe_pkd_glu_silu_kernel(
@@ -82,14 +83,15 @@ def tile_moe_pkd_glu_silu_kernel(
                 )
             return codes, scales
 
-        def round_first(raw, name, share):
+        def round_first(raw, name, share, pieces=1):
             rounded = work.tile([P, H * PACK], BF16, name=name, align_bytes=64)
             dst = rounded[:].rearrange("p (t m u v) -> p m u t v", t=PACK, u=2, v=2)
             src = raw[:, 0].rearrange("p (u v) (m t) -> p m u t v", t=PACK, u=2)
             if share > 0:
                 on_scalar(dst[:, :share], src[:, :share])
             if share < P:
-                on_vector(dst[:, share:], src[:, share:])
+                for t in range(0, PACK, PACK // pieces):
+                    on_vector(dst[:, share:, :, t : t + PACK // pieces], src[:, share:, :, t : t + PACK // pieces])
             return rounded
 
         def first_product(weights, e, name):
@@ -204,7 +206,7 @@ def tile_moe_pkd_glu_silu_kernel(
                 quantize_w2(EARLY_W2[e - 1], rounded2, "w2", 1)
             if e == LAST:
                 quantize_w2(BETWEEN, round_w2(BETWEEN, raw_between, "late_w2", LATE_BUFS), "late_w2", LATE_BUFS)
-            rounded3 = round_first(raw3, "rounded3", W3_SHARE.get(e, P))
+            rounded3 = round_first(raw3, "rounded3", W3_SHARE.get(e, P), pieces=2 if e == LAST else 1)
             silu_a[e] = raw3[:, 0, :, :C].rearrange("p q (c t) -> p q c t", t=PACK)
             nc.scalar.activation(silu_a[e], a[:].rearrange("p t (q c) -> p q c t", q=PACK), SILU)
             w3_mx = quantize(rounded3[:], H, "w3", pieces=2 if e == LAST else 1)
@@ -227,24 +229,14 @@ def tile_moe_pkd_glu_silu_kernel(
             gates[t0] = stream.tile([P, TOP, RANGE], F32, name="gates", tag="raw", align_bytes=64)
             nc.sync.dma_start(gates[t0][:], gate[:, :, t0 : t0 + RANGE].rearrange("r p t -> p r t"))
 
-        by_expert = y[:].rearrange("p (e c) -> p e c", c=C)
-
-        late = [e for group in LATE_LOADS for e in group]
-        late_rounded = {}
+        last_h = keep.tile([P, C * PACK], BF16, name="last_h", align_bytes=64)
+        multiply(LAST, last_h[:])
+        h_mx[LAST] = quantize(last_h[:], C, "h", bufs=H_BUFS)
         for group in LATE_LOADS:
             for g, e in enumerate(group):
-                name, bufs = ("held", 1) if e == LAST - 1 else ("late_w2", LATE_BUFS)
-                late_rounded[e] = round_w2((e,), late_raw[group][:, g : g + 1], name, bufs)
-        quantize_w2(late[:1], late_rounded[late[0]], "late_w2", LATE_BUFS)
-        last_h = late_rounded[late[0]][:]
-        multiply(LAST, last_h)
-        for e in late[1:-1]:
-            quantize_w2((e,), late_rounded[e], "late_w2", LATE_BUFS)
-        last_codes = work.tile([P, C], U32, name="held", align_bytes=64, bufs=1)
-        last_scales = work.tile([P, C], U8, name="last_scales", align_bytes=64, bufs=1)
-        nc.vector.quantize_mx(out=last_codes[:].bitcast(FP8X4), scales=last_scales[:], in_=last_h)
-        h_mx[LAST] = (last_codes, last_scales)
-        quantize_w2((LAST,), late_rounded[LAST], "late_w2", LATE_BUFS)
+                late_rounded = round_w2((e,), late_raw[group][:, g : g + 1], "late_w2", LATE_BUFS)
+                quantize_w2((e,), late_rounded, "late_w2", LATE_BUFS)
+        by_expert = y[:].rearrange("p (e c) -> p e c", c=C)
         inner = LATE_W2[1:-1]
         outer_acc = psum.tile([P, 2, C], F32, name="y_acc")
         inner_acc = psum.tile([P, len(inner), C], F32, name="y_acc")
@@ -255,21 +247,20 @@ def tile_moe_pkd_glu_silu_kernel(
         on_scalar(by_expert[:, inner[0] : LAST, :], inner_acc[:])
         on_vector(by_expert[:, LATE_W2[0] :: LAST - LATE_W2[0], :], outer_acc[:])
 
-        def offsets_of(r, lo, hi):
-            return back_lists[r][:, lo // LIST_ROWS : hi // LIST_ROWS]
+        def looked_up(r, t0):
+            return y[:].indirect(back_lists[r][:, t0 // LIST_ROWS : (t0 + RANGE) // LIST_ROWS])
 
         early, middle, late = range(0, T, RANGE)
         plain, parts = {}, {}
-        for r, t0 in ((2, early), (1, middle), (2, middle), (1, late), (2, late)):
-            plain[r, t0] = keep.tile([P, RANGE], F32, name="plain%d_%d" % (r, t0))
-            nc.scalar.activation(plain[r, t0][:], y[:].indirect(offsets_of(r, t0, t0 + RANGE)), COPY)
-        for t0, r in [(t0, r) for t0 in (early, middle, late) for r in range(TOP)]:
-            parts[r, t0] = keep.tile([P, RANGE], F32, name="part%d_%d" % (r, t0))
-            if (r, t0) in plain:
-                fetched = plain[r, t0][:]
-            else:
-                fetched = y[:].indirect(offsets_of(r, t0, t0 + RANGE))
-            nc.vector.tensor_tensor(parts[r, t0][:], fetched, gates[t0][:, r, :], MULT)
+        for t0, fused in zip((early, middle, late), FUSED):
+            for r in range(fused, TOP):
+                plain[r, t0] = keep.tile([P, RANGE], F32, name="plain%d_%d" % (r, t0))
+                nc.scalar.activation(plain[r, t0][:], looked_up(r, t0), COPY)
+        for t0 in (early, middle, late):
+            for r in range(TOP):
+                parts[r, t0] = keep.tile([P, RANGE], F32, name="part%d_%d" % (r, t0))
+                fetched = plain[r, t0][:] if (r, t0) in plain else looked_up(r, t0)
+                nc.vector.tensor_tensor(parts[r, t0][:], fetched, gates[t0][:, r, :], MULT)
 
         blocks = RANGE // P
         sums, back_turned = {}, {}

@@ -24,17 +24,21 @@ P = 128
 PACK = 4
 LIST_ROWS = 16
 LAST = E - 1
-GATHER_EXPERTS = 3
-GATHER_BUFS = 3
-W1_SHARE = {LAST: 40}
-W3_SHARE = {LAST - 1: 88, LAST: C // PACK}
-EARLY_W2 = {0: (0, 1, 2, 3), 3: (4, 5, 6, 7), 7: (8, 9, 10, 11)}
-BETWEEN = (12, 13)
-LATE_LOADS = ((14, 15), (16, 17))
-LATE_W2 = tuple(range(12, E))
-LATE_BUFS = 5
-H_BUFS = len(LATE_W2) + 2
+BURST = 256
+GATHER_EXPERTS = 2
 STREAM_BUFS = 14
+SLOT = H * PACK * 4 + C * PACK * 2
+H_OVERLAP = 32
+ROUNDED = H * PACK * 2
+ROUNDED_SLOTS = 8
+W1_SHARE = {15: 48, 16: 48, 17: 48}
+W3_SHARE = {14: 96, 15: 72, 16: 72, LAST: 56}
+EARLY_W2 = {1: (0, 1), 3: (2, 3), 5: (4, 5), 7: (6, 7), 9: (8, 9), 11: (10, 11)}
+EARLY_BANKS = ((0, 1, 2, 3), (4, 5, 6, 7), (8, 9, 10, 11))
+LATE_W2 = ((12, 13), (14, 15), (16,), (17,))
+W2_ON_VECTOR = (12, 13)
+LATE_BANKS = ((12, 13, 14, 15), (16, 17))
+Y_ON_VECTOR = (16,)
 WARM_PASSES = 4
 RANGE = 256
 FUSED = (2, 1, 1)
@@ -45,8 +49,9 @@ def tile_moe_pkd_glu_silu_kernel(
 ):
     nc = tc.nc
     with ExitStack() as ctx:
+        stream = ctx.enter_context(tc.tile_pool(name="stream", bufs=1))
+        rounds = ctx.enter_context(tc.tile_pool(name="rounds", bufs=1))
         keep = ctx.enter_context(tc.tile_pool(name="keep", bufs=1))
-        stream = ctx.enter_context(tc.tile_pool(name="stream", bufs=STREAM_BUFS))
         work = ctx.enter_context(tc.tile_pool(name="work", bufs=2))
         psum = ctx.enter_context(tc.psum_pool(name="psum", bufs=2))
 
@@ -55,21 +60,30 @@ def tile_moe_pkd_glu_silu_kernel(
         make_identity(nc, identity[:])
         on_scalar, on_vector = nc.scalar.copy, nc.vector.tensor_copy
 
+        ring = []
+
+        def ring_tile(shape):
+            start = len(ring) % STREAM_BUFS * SLOT
+            ring.append(start)
+            return stream.tile(shape, F32, name="raw%d" % len(ring), align_bytes=BURST, offset=start)
+
         def load(weights, experts):
-            raw = stream.tile([P, len(experts), PACK, weights.shape[2]], F32, name="raw", align_bytes=64)
+            raw = ring_tile([P, len(experts), PACK, weights.shape[2]])
             nc.sync.dma_start(
                 raw[:], weights[experts[0] : experts[-1] + 1].rearrange("g (p j) c -> p g j c", j=PACK)
             )
             return raw
 
-        def gather_tokens(g):
+        def rounded_start(e):
+            return e % ROUNDED_SLOTS * ROUNDED
+
+        def gather(g, table, dtype, e):
             width = GATHER_EXPERTS * C
             offsets = slot_list[:, g * width // LIST_ROWS : (g + 1) * width // LIST_ROWS]
-            words = work.tile([P, width], U32, name="slot_words", align_bytes=64, bufs=GATHER_BUFS)
-            scales = work.tile([P, width], U8, name="slot_scales", align_bytes=64, bufs=GATHER_BUFS)
-            nc.vector.tensor_copy(words[:], token_words[:].bitcast(U32).indirect(offsets))
-            nc.vector.tensor_copy(scales[:], token_scales[:].bitcast(U8).indirect(offsets))
-            return words, scales
+            start = rounded_start(e)
+            picked = rounds.tile([P, width], dtype, name="picked%d" % (e + 4), align_bytes=64, offset=start)
+            nc.vector.tensor_copy(picked[:], table[:].bitcast(dtype).indirect(offsets))
+            return picked
 
         def quantize(rounded, width, name, bufs=2, pieces=1):
             codes = work.tile([P, width], U32, name=name + "_codes", align_bytes=64, bufs=bufs)
@@ -83,16 +97,16 @@ def tile_moe_pkd_glu_silu_kernel(
                 )
             return codes, scales
 
-        def round_first(raw, name, share, pieces=1):
-            rounded = work.tile([P, H * PACK], BF16, name=name, align_bytes=64)
+        def round_first(raw, rounded, share, pieces=1):
             dst = rounded[:].rearrange("p (t m u v) -> p m u t v", t=PACK, u=2, v=2)
             src = raw[:, 0].rearrange("p (u v) (m t) -> p m u t v", t=PACK, u=2)
             if share > 0:
-                on_scalar(dst[:, :share], src[:, :share])
+                on_scalar(dst[:, P - share :], src[:, P - share :])
             if share < P:
                 for t in range(0, PACK, PACK // pieces):
-                    on_vector(dst[:, share:, :, t : t + PACK // pieces], src[:, share:, :, t : t + PACK // pieces])
-            return rounded
+                    on_vector(
+                        dst[:, : P - share, :, t : t + PACK // pieces], src[:, : P - share, :, t : t + PACK // pieces]
+                    )
 
         def first_product(weights, e, name):
             words, scales = tokens[e // GATHER_EXPERTS]
@@ -133,27 +147,30 @@ def tile_moe_pkd_glu_silu_kernel(
                 MULT,
             )
 
-        def round_w2(experts, raw, name, bufs):
-            count = len(experts)
-            rounded = work.tile([P, count * N * PACK], BF16, name=name, align_bytes=64, bufs=bufs)
-            for g in range(count):
-                on_scalar(
-                    rounded[:, g * N * PACK : (g + 1) * N * PACK].rearrange(
-                        "p (m s u v) -> p m u s v", s=PACK, u=2, v=2
-                    ),
-                    raw[:, g].rearrange("p (u v) (m s) -> p m u s v", s=PACK, u=2),
-                )
+        def round_w2(e, raw, rounded):
+            copy = on_vector if e in W2_ON_VECTOR else on_scalar
+            copy(
+                rounded.rearrange("p (m s u v) -> p m u s v", s=PACK, u=2, v=2),
+                raw.rearrange("p (u v) (m s) -> p m u s v", s=PACK, u=2),
+            )
+
+        def round_group(group, raw):
+            rounded = work.tile([P, len(group) * N * PACK], BF16, name="rounded2", align_bytes=64, bufs=1)
+            for g, e in enumerate(group):
+                round_w2(e, raw[:, g], rounded[:, g * N * PACK : (g + 1) * N * PACK])
             return rounded
 
-        def quantize_w2(experts, rounded, name, bufs):
-            count = len(experts)
-            codes, scales = quantize(rounded[:], count * N, name, bufs)
-            for g, e in enumerate(experts):
+        def quantize_group(group, rounded):
+            codes, scales = quantize(rounded, len(group) * N, "w2_%d" % group[0], 1)
+            for g, e in enumerate(group):
                 w2_mx[e] = (codes[:, g * N : (g + 1) * N], scales[:, g * N : (g + 1) * N])
 
-        def second_product(e, place):
+        def second_product(e):
+            bank = [x for x in EARLY_BANKS + LATE_BANKS if e in x][0]
+            if e == bank[0]:
+                banks[bank] = psum.tile([P, len(bank), C], F32, name="y_acc")
             nc.tensor.matmul_mx(
-                out=place,
+                out=banks[bank][:, e - bank[0], :],
                 lhsT=w2_mx[e][0].bitcast(FP8X4),
                 lhsT_scale=w2_mx[e][1],
                 rhs=h_mx[e][0][:].bitcast(FP8X4),
@@ -161,64 +178,80 @@ def tile_moe_pkd_glu_silu_kernel(
                 start=True,
                 stop=True,
             )
+            if e == bank[-1]:
+                copy = on_vector if bank[0] in Y_ON_VECTOR else on_scalar
+                copy(y[:, bank[0] * C : (e + 1) * C], banks[bank][:].rearrange("p g c -> p (g c)"))
 
+        banks = {}
         tokens, b, silu_a, h_mx, w2_mx = {}, {}, {}, {}, {}
-        raw1 = load(w1, (0,))
+        def load_w1(e):
+            slot1 = ring_tile([P, SLOT // 4])
+            nc.sync.dma_start(slot1[:, : H * PACK], w1[e].rearrange("(p j) c -> p (j c)", j=PACK))
+            return slot1
+
+        slot1 = load_w1(0)
         slot_list = keep.tile([P, S // LIST_ROWS], U16, name="slot_list")
         nc.sync.dma_start(slot_list[:], offs)
-        token_words = keep.tile([P, T], I32, name="token_words")
+        token_words = keep.tile([P, T], I32, name="token_words", align_bytes=BURST)
         nc.sync.dma_start(token_words[:], x_words[0].rearrange("p t r -> p (t r)").bitcast(I32))
         token_scales = keep.tile([P, T // 4], I32, name="token_scales")
-        loaded_scales = keep.tile([P, T // 4], I32, name="loaded_scales")
+        loaded_scales = keep.tile([P, T // 4], I32, name="loaded_scales", align_bytes=BURST)
         nc.vector.memset(token_scales[:], 0)
         for quadrant in range(4):
             rows = slice(32 * quadrant, 32 * quadrant + 4)
             nc.sync.dma_start(loaded_scales[rows, :], x_scales[0, 4 * quadrant : 4 * quadrant + 4, :].bitcast(I32))
             nc.vector.tensor_copy(token_scales[rows, :], loaded_scales[rows, :])
+
+        for g in range(2):
+            tokens[g] = gather(g, token_words, U32, 2 * g - 4), gather(g, token_scales, U8, 2 * g - 3)
+        rounded3 = {}
         for e in range(E):
             if e > 0:
-                raw1 = load(w1, (e,))
-            if e == LAST:
-                raw_between = load(w2, BETWEEN)
+                slot1 = load_w1(e)
+            raw1 = slot1[:, : H * PACK].rearrange("p (g j c) -> p g j c", g=1, j=PACK)
             raw3 = load(w3, (e,))
             if e in EARLY_W2:
                 raw2 = load(w2, EARLY_W2[e])
-            if e % GATHER_EXPERTS == 0:
-                tokens[e // GATHER_EXPERTS] = gather_tokens(e // GATHER_EXPERTS)
-            rounded1 = round_first(raw1, "rounded1", W1_SHARE.get(e, 0))
-            w1_mx = quantize(rounded1[:], H, "w1")
-            a = first_product(w1_mx, e, "a")
+            rounded1 = rounds.tile(
+                [P, H * PACK], BF16, name="rounded1_%d" % e, align_bytes=64, offset=rounded_start(e)
+            )
+            round_first(raw1, rounded1, W1_SHARE.get(e, 24))
             if e > 0:
-                h = raw1[:, 0, 0, : C * PACK // 2].bitcast(BF16)
+                b[e - 1] = first_product(quantize(rounded3[e - 1][:], H, "w3"), e - 1, "b")
+                start = H * PACK - H_OVERLAP
+                h = slot1[:, start : start + C * PACK // 2].bitcast(BF16)
                 multiply(e - 1, h)
+            w1_mx = quantize(rounded1[:], H, "w1", bufs=1)
+            a = first_product(w1_mx, e, "a")
             if e == LAST:
                 warm_up(w1_mx)
+            if e - 1 in EARLY_W2:
+                quantize_group(EARLY_W2[e - 1], rounded2[:])
             if e > 0:
-                h_mx[e - 1] = quantize(h, C, "h", bufs=H_BUFS)
-                if e - 1 not in LATE_W2:
-                    group = [x for x in EARLY_W2.values() if e - 1 in x][0]
-                    if e - 1 == group[0]:
-                        group_acc = psum.tile([P, len(group), C], F32, name="y_acc")
-                    second_product(e - 1, group_acc[:, e - 1 - group[0], :])
-                    if e - 1 == group[-1]:
-                        on_scalar(y[:, group[0] * C : e * C], group_acc[:].rearrange("p g c -> p (g c)"))
-            if e - 1 in EARLY_W2 and e > 1:
-                quantize_w2(EARLY_W2[e - 1], rounded2, "w2", 1)
-            if e == LAST:
-                quantize_w2(BETWEEN, round_w2(BETWEEN, raw_between, "late_w2", LATE_BUFS), "late_w2", LATE_BUFS)
-            rounded3 = round_first(raw3, "rounded3", W3_SHARE.get(e, P), pieces=2 if e == LAST else 1)
-            silu_a[e] = raw3[:, 0, :, :C].rearrange("p q (c t) -> p q c t", t=PACK)
+                h_mx[e - 1] = quantize(h, C, "h", bufs=E)
+            for x in EARLY_W2.get(e - 1, ()):
+                second_product(x)
+            following = e // GATHER_EXPERTS + 2
+            if following < E // GATHER_EXPERTS:
+                if e % GATHER_EXPERTS == 0:
+                    words = gather(following, token_words, U32, e)
+                else:
+                    tokens[following] = words, gather(following, token_scales, U8, e)
+            rounded3[e] = work.tile([P, H * PACK], BF16, name="rounded3", align_bytes=64)
+            round_first(raw3, rounded3[e], W3_SHARE.get(e, P), pieces=2 if e == LAST else 1)
+            if e < LAST:
+                silu_a[e] = raw3[:, 0, :, H - C :].rearrange("p q (c t) -> p q c t", t=PACK)
+            else:
+                last_silu = work.tile([P, PACK, C], F32, name="last_silu", align_bytes=64, bufs=1)
+                silu_a[e] = last_silu[:].rearrange("p q (c t) -> p q c t", t=PACK)
             nc.scalar.activation(silu_a[e], a[:].rearrange("p t (q c) -> p q c t", q=PACK), SILU)
-            w3_mx = quantize(rounded3[:], H, "w3", pieces=2 if e == LAST else 1)
-            b[e] = first_product(w3_mx, e, "b")
-            if e == LAST:
-                warm_up(w3_mx)
             if e in EARLY_W2:
-                rounded2 = round_w2(EARLY_W2[e], raw2, "w2", 1)
-                if e == 0:
-                    quantize_w2(EARLY_W2[e], rounded2, "w2", 1)
+                rounded2 = round_group(EARLY_W2[e], raw2)
+        w3_mx = quantize(rounded3[LAST][:], H, "w3", pieces=2)
+        b[LAST] = first_product(w3_mx, LAST, "b")
+        warm_up(w3_mx)
 
-        late_raw = {group: load(w2, group) for group in LATE_LOADS}
+        late_raw = {group: load(w2, group) for group in LATE_W2}
         back_lists = []
         for r, pos in enumerate((pos1, pos2, pos3)):
             back = keep.tile([P, T // LIST_ROWS], U16, name="back_list%d" % r)
@@ -226,26 +259,34 @@ def tile_moe_pkd_glu_silu_kernel(
             back_lists.append(back)
         gates = {}
         for t0 in range(0, T, RANGE):
-            gates[t0] = stream.tile([P, TOP, RANGE], F32, name="gates", tag="raw", align_bytes=64)
+            gates[t0] = ring_tile([P, TOP, RANGE])
             nc.sync.dma_start(gates[t0][:], gate[:, :, t0 : t0 + RANGE].rearrange("r p t -> p r t"))
 
         last_h = keep.tile([P, C * PACK], BF16, name="last_h", align_bytes=64)
         multiply(LAST, last_h[:])
-        h_mx[LAST] = quantize(last_h[:], C, "h", bufs=H_BUFS)
-        for group in LATE_LOADS:
-            for g, e in enumerate(group):
-                late_rounded = round_w2((e,), late_raw[group][:, g : g + 1], "late_w2", LATE_BUFS)
-                quantize_w2((e,), late_rounded, "late_w2", LATE_BUFS)
-        by_expert = y[:].rearrange("p (e c) -> p e c", c=C)
-        inner = LATE_W2[1:-1]
-        outer_acc = psum.tile([P, 2, C], F32, name="y_acc")
-        inner_acc = psum.tile([P, len(inner), C], F32, name="y_acc")
-        second_product(LATE_W2[0], outer_acc[:, 0, :])
-        for g, e in enumerate(inner):
-            second_product(e, inner_acc[:, g, :])
-        second_product(LAST, outer_acc[:, 1, :])
-        on_scalar(by_expert[:, inner[0] : LAST, :], inner_acc[:])
-        on_vector(by_expert[:, LATE_W2[0] :: LAST - LATE_W2[0], :], outer_acc[:])
+        h_mx[LAST] = quantize(last_h[:], C, "h", bufs=E)
+
+        raw_of = {e: late_raw[group][:, g] for group in LATE_W2 for g, e in enumerate(group)}
+        width = N * PACK
+        place = {e: keep.tile([P, width], BF16, name="late_rounded%d" % e, align_bytes=64)[:] for e in raw_of}
+
+        def quantize_late(e):
+            codes = keep.tile([P, N], U32, name="late_codes%d" % e, align_bytes=64)[:]
+            scales = keep.tile([P, N], U8, name="late_scales%d" % e, align_bytes=64)
+            nc.vector.quantize_mx(out=codes.bitcast(FP8X4), scales=scales[:], in_=place[e])
+            w2_mx[e] = (codes, scales[:])
+            second_product(e)
+
+        for e in raw_of:
+            round_w2(e, raw_of[e], place[e])
+            quantize_late(e)
+
+        spare = []
+
+        def spare_tile(width):
+            start = sum(spare)
+            spare.append(4 * RANGE)
+            return rounds.tile([P, width], F32, name="spare%d" % len(spare), align_bytes=BURST, offset=start)
 
         def looked_up(r, t0):
             return y[:].indirect(back_lists[r][:, t0 // LIST_ROWS : (t0 + RANGE) // LIST_ROWS])
@@ -254,11 +295,11 @@ def tile_moe_pkd_glu_silu_kernel(
         plain, parts = {}, {}
         for t0, fused in zip((early, middle, late), FUSED):
             for r in range(fused, TOP):
-                plain[r, t0] = keep.tile([P, RANGE], F32, name="plain%d_%d" % (r, t0))
+                plain[r, t0] = spare_tile(RANGE)
                 nc.scalar.activation(plain[r, t0][:], looked_up(r, t0), COPY)
         for t0 in (early, middle, late):
             for r in range(TOP):
-                parts[r, t0] = keep.tile([P, RANGE], F32, name="part%d_%d" % (r, t0))
+                parts[r, t0] = spare_tile(RANGE)
                 fetched = plain[r, t0][:] if (r, t0) in plain else looked_up(r, t0)
                 nc.vector.tensor_tensor(parts[r, t0][:], fetched, gates[t0][:, r, :], MULT)
 
@@ -279,12 +320,12 @@ def tile_moe_pkd_glu_silu_kernel(
                 on_scalar(turned[:], sums[t0][blk][:])
                 nc.tensor.transpose(back_turned[t0][:, blk, :], turned[:], identity[:])
         for t0, queue in ((early, nc.sync), (middle, nc.scalar)):
-            head = keep.tile([P, RANGE], F32, name="head%d" % t0)
+            head = spare_tile(RANGE)
             on_scalar(head[:], back_turned[t0][:].rearrange("p blk c -> p (blk c)"))
             queue.dma_start(out[:, t0 : t0 + RANGE], head[:])
 
-        pair = keep.tile([P, RANGE], F32, name="pair")
-        rest = keep.tile([P, RANGE], F32, name="rest")
+        pair = spare_tile(RANGE)
+        rest = spare_tile(RANGE)
         for total, first, second in ((pair, parts[0, late], parts[1, late]), (rest, pair, parts[2, late])):
             for blk in range(blocks):
                 cols = slice(blk * P, (blk + 1) * P)

@@ -1,3 +1,4 @@
+import math
 from contextlib import ExitStack
 
 import concourse.mybir as mybir
@@ -25,20 +26,23 @@ PACK = 4
 LIST_ROWS = 16
 LAST = E - 1
 BURST = 256
-GATHER_EXPERTS = 2
-STREAM_BUFS = 14
+GATHER_EXPERTS = 3
+RING = 88 * 1024
+PAIRED = 10
+FIRST_SHARE = 48
 SLOT = H * PACK * 4 + C * PACK * 2
 H_OVERLAP = 32
 ROUNDED = H * PACK * 2
-ROUNDED_SLOTS = 8
-W1_SHARE = {15: 48, 16: 48, 17: 48}
-W3_SHARE = {14: 96, 15: 72, 16: 72, LAST: 56}
-EARLY_W2 = {1: (0, 1), 3: (2, 3), 5: (4, 5), 7: (6, 7), 9: (8, 9), 11: (10, 11)}
+ROUNDED_SLOTS = 12
+W1_SHARE = {LAST: 40}
+W3_SHARE = {10: 80, LAST - 1: 88, LAST: 48}
+EARLY_W2 = {5: (0, 1, 2, 3), 9: (4, 5, 6, 7), 12: (8, 9, 10, 11)}
 EARLY_BANKS = ((0, 1, 2, 3), (4, 5, 6, 7), (8, 9, 10, 11))
-LATE_W2 = ((12, 13), (14, 15), (16,), (17,))
-W2_ON_VECTOR = (12, 13)
-LATE_BANKS = ((12, 13, 14, 15), (16, 17))
-Y_ON_VECTOR = (16,)
+BETWEEN = (12, 13)
+LATE_W2 = ((14, 15), (16, 17))
+W2_ON_VECTOR = (14,)
+LATE_BANKS = ((13, 14, 15, 16), (12, 17))
+Y_ON_VECTOR = (12,)
 WARM_PASSES = 4
 RANGE = 256
 FUSED = (2, 1, 1)
@@ -60,11 +64,12 @@ def tile_moe_pkd_glu_silu_kernel(
         make_identity(nc, identity[:])
         on_scalar, on_vector = nc.scalar.copy, nc.vector.tensor_copy
 
-        ring = []
+        ring = [0]
 
         def ring_tile(shape):
-            start = len(ring) % STREAM_BUFS * SLOT
-            ring.append(start)
+            size = 4 * math.prod(shape[1:])
+            start = ring[-1] if ring[-1] + size <= RING else 0
+            ring.append(start + size)
             return stream.tile(shape, F32, name="raw%d" % len(ring), align_bytes=BURST, offset=start)
 
         def load(weights, experts):
@@ -77,13 +82,15 @@ def tile_moe_pkd_glu_silu_kernel(
         def rounded_start(e):
             return e % ROUNDED_SLOTS * ROUNDED
 
-        def gather(g, table, dtype, e):
+        def gather(g, slot):
             width = GATHER_EXPERTS * C
             offsets = slot_list[:, g * width // LIST_ROWS : (g + 1) * width // LIST_ROWS]
-            start = rounded_start(e)
-            picked = rounds.tile([P, width], dtype, name="picked%d" % (e + 4), align_bytes=64, offset=start)
-            nc.vector.tensor_copy(picked[:], table[:].bitcast(dtype).indirect(offsets))
-            return picked
+            start = rounded_start(slot)
+            words = rounds.tile([P, width], U32, name="words%d" % g, align_bytes=64, offset=start)
+            scales = rounds.tile([P, width], U8, name="scales%d" % g, align_bytes=64, offset=start + 4 * width)
+            nc.vector.tensor_copy(words[:], token_words[:].bitcast(U32).indirect(offsets))
+            nc.vector.tensor_copy(scales[:], token_scales[:].bitcast(U8).indirect(offsets))
+            return words, scales
 
         def quantize(rounded, width, name, bufs=2, pieces=1):
             codes = work.tile([P, width], U32, name=name + "_codes", align_bytes=64, bufs=bufs)
@@ -98,8 +105,8 @@ def tile_moe_pkd_glu_silu_kernel(
             return codes, scales
 
         def round_first(raw, rounded, share, pieces=1):
-            dst = rounded[:].rearrange("p (t m u v) -> p m u t v", t=PACK, u=2, v=2)
-            src = raw[:, 0].rearrange("p (u v) (m t) -> p m u t v", t=PACK, u=2)
+            dst = rounded.rearrange("p (t m u v) -> p m u t v", t=PACK, u=2, v=2)
+            src = raw.rearrange("p (u v) (m t) -> p m u t v", t=PACK, u=2)
             if share > 0:
                 on_scalar(dst[:, P - share :], src[:, P - share :])
             if share < P:
@@ -170,7 +177,7 @@ def tile_moe_pkd_glu_silu_kernel(
             if e == bank[0]:
                 banks[bank] = psum.tile([P, len(bank), C], F32, name="y_acc")
             nc.tensor.matmul_mx(
-                out=banks[bank][:, e - bank[0], :],
+                out=banks[bank][:, bank.index(e), :],
                 lhsT=w2_mx[e][0].bitcast(FP8X4),
                 lhsT_scale=w2_mx[e][1],
                 rhs=h_mx[e][0][:].bitcast(FP8X4),
@@ -180,12 +187,13 @@ def tile_moe_pkd_glu_silu_kernel(
             )
             if e == bank[-1]:
                 copy = on_vector if bank[0] in Y_ON_VECTOR else on_scalar
-                copy(y[:, bank[0] * C : (e + 1) * C], banks[bank][:].rearrange("p g c -> p (g c)"))
+                copy(by_expert[:, bank[0] : e + 1 : bank[1] - bank[0], :], banks[bank][:])
 
         banks = {}
+        by_expert = y[:].rearrange("p (e c) -> p e c", c=C)
         tokens, b, silu_a, h_mx, w2_mx = {}, {}, {}, {}, {}
         def load_w1(e):
-            slot1 = ring_tile([P, SLOT // 4])
+            slot1 = ring_tile([P, H * PACK])
             nc.sync.dma_start(slot1[:, : H * PACK], w1[e].rearrange("(p j) c -> p (j c)", j=PACK))
             return slot1
 
@@ -198,53 +206,98 @@ def tile_moe_pkd_glu_silu_kernel(
         loaded_scales = keep.tile([P, T // 4], I32, name="loaded_scales", align_bytes=BURST)
         nc.vector.memset(token_scales[:], 0)
         for quadrant in range(4):
+            nc.sync.dma_start(loaded_scales[quadrant:P:32, :], x_scales[0, quadrant:16:4, :].bitcast(I32))
+        for quadrant in range(4):
             rows = slice(32 * quadrant, 32 * quadrant + 4)
-            nc.sync.dma_start(loaded_scales[rows, :], x_scales[0, 4 * quadrant : 4 * quadrant + 4, :].bitcast(I32))
             nc.vector.tensor_copy(token_scales[rows, :], loaded_scales[rows, :])
 
-        for g in range(2):
-            tokens[g] = gather(g, token_words, U32, 2 * g - 4), gather(g, token_scales, U8, 2 * g - 3)
-        rounded3 = {}
-        for e in range(E):
+        def rounded_tile(e, count):
+            return rounds.tile(
+                [P, count * H * PACK], BF16, name="rounded1_%d" % e, align_bytes=64, offset=rounded_start(e)
+            )
+
+        def apply_silu(e, place):
+            silu_a[e] = place.rearrange("p q (c t) -> p q c t", t=PACK)
+            nc.scalar.activation(silu_a[e], a[e][:].rearrange("p t (q c) -> p q c t", q=PACK), SILU)
+
+        def hidden(e):
+            h = work.tile([P, C * PACK], BF16, name="h", align_bytes=64)
+            multiply(e, h[:])
+            h_mx[e] = quantize(h[:], C, "h", bufs=E)
+
+        def halves(mx):
+            return [(mx[0][:, g * H : (g + 1) * H], mx[1][:, g * H : (g + 1) * H]) for g in range(2)]
+
+        def finish_group(group, rounded):
+            quantize_group(group, rounded[:])
+            for x in group:
+                second_product(x)
+
+        for g, slot in enumerate((7, 9, 11)):
+            tokens[g] = gather(g, slot)
+        a, rounded3 = {}, {}
+        rounded1 = rounded_tile(0, 1)
+        round_first(slot1[:, : H * PACK].rearrange("p (j c) -> p j c", j=PACK), rounded1[:], 0)
+        a[0] = first_product(quantize(rounded1[:], H, "w1"), 0, "a")
+        for e in range(0, PAIRED, 2):
+            pair3 = load(w3, (e, e + 1))
+            both = work.tile([P, 2 * H * PACK], BF16, name="rounded3", align_bytes=64)
+            round_first(pair3[:, 0], both[:, : H * PACK], FIRST_SHARE)
+            round_first(pair3[:, 1], both[:, H * PACK :], P)
             if e > 0:
+                apply_silu(e - 1, pair3[:, 0, :, :C])
+            apply_silu(e, pair3[:, 0, :, H - C :])
+            if e > 0:
+                hidden(e - 1)
+            for g, mx in enumerate(halves(quantize(both[:], 2 * H, "w3"))):
+                b[e + g] = first_product(mx, e + g, "b")
+            if e - 1 in EARLY_W2:
+                finish_group(EARLY_W2[e - 1], rounded2)
+            pair1 = load(w1, (e + 1, e + 2))
+            if e + 1 in EARLY_W2:
+                raw2 = load(w2, EARLY_W2[e + 1])
+            both = rounded_tile(e + 1, 2)
+            round_first(pair1[:, 0], both[:, : H * PACK], 0)
+            round_first(pair1[:, 1], both[:, H * PACK :], P)
+            hidden(e)
+            for g, mx in enumerate(halves(quantize(both[:], 2 * H, "w1"))):
+                a[e + 1 + g] = first_product(mx, e + 1 + g, "a")
+            if e // 2 + 3 < E // GATHER_EXPERTS:
+                tokens[e // 2 + 3] = gather(e // 2 + 3, e + 2)
+            if e + 1 in EARLY_W2:
+                rounded2 = round_group(EARLY_W2[e + 1], raw2)
+        for e in range(PAIRED, E):
+            if e > PAIRED:
                 slot1 = load_w1(e)
-            raw1 = slot1[:, : H * PACK].rearrange("p (g j c) -> p g j c", g=1, j=PACK)
-            raw3 = load(w3, (e,))
+            if e == LAST:
+                raw_between = load(w2, BETWEEN)
+            raw3 = load(w3, (e,))[:, 0]
             if e in EARLY_W2:
                 raw2 = load(w2, EARLY_W2[e])
-            rounded1 = rounds.tile(
-                [P, H * PACK], BF16, name="rounded1_%d" % e, align_bytes=64, offset=rounded_start(e)
-            )
-            round_first(raw1, rounded1, W1_SHARE.get(e, 24))
-            if e > 0:
+            if e > PAIRED:
+                rounded1 = rounded_tile(e, 1)
+                raw1 = slot1[:, : H * PACK].rearrange("p (j c) -> p j c", j=PACK)
+                round_first(raw1, rounded1[:], W1_SHARE.get(e, 0))
                 b[e - 1] = first_product(quantize(rounded3[e - 1][:], H, "w3"), e - 1, "b")
-                start = H * PACK - H_OVERLAP
-                h = slot1[:, start : start + C * PACK // 2].bitcast(BF16)
+                h = slot1[:, : C * PACK // 2].bitcast(BF16)
+                w1_mx = quantize(rounded1[:], H, "w1")
+                a[e] = first_product(w1_mx, e, "a")
                 multiply(e - 1, h)
-            w1_mx = quantize(rounded1[:], H, "w1", bufs=1)
-            a = first_product(w1_mx, e, "a")
-            if e == LAST:
-                warm_up(w1_mx)
-            if e - 1 in EARLY_W2:
-                quantize_group(EARLY_W2[e - 1], rounded2[:])
-            if e > 0:
+                if e == LAST:
+                    warm_up(w1_mx)
                 h_mx[e - 1] = quantize(h, C, "h", bufs=E)
-            for x in EARLY_W2.get(e - 1, ()):
-                second_product(x)
-            following = e // GATHER_EXPERTS + 2
-            if following < E // GATHER_EXPERTS:
-                if e % GATHER_EXPERTS == 0:
-                    words = gather(following, token_words, U32, e)
-                else:
-                    tokens[following] = words, gather(following, token_scales, U8, e)
+                if e - 1 in EARLY_W2:
+                    finish_group(EARLY_W2[e - 1], rounded2)
+            if e == LAST:
+                quantize_group(BETWEEN, round_group(BETWEEN, raw_between)[:])
             rounded3[e] = work.tile([P, H * PACK], BF16, name="rounded3", align_bytes=64)
-            round_first(raw3, rounded3[e], W3_SHARE.get(e, P), pieces=2 if e == LAST else 1)
-            if e < LAST:
-                silu_a[e] = raw3[:, 0, :, H - C :].rearrange("p q (c t) -> p q c t", t=PACK)
-            else:
-                last_silu = work.tile([P, PACK, C], F32, name="last_silu", align_bytes=64, bufs=1)
-                silu_a[e] = last_silu[:].rearrange("p q (c t) -> p q c t", t=PACK)
-            nc.scalar.activation(silu_a[e], a[:].rearrange("p t (q c) -> p q c t", q=PACK), SILU)
+            round_first(raw3, rounded3[e][:], W3_SHARE.get(e, P), pieces=2 if e == LAST else 1)
+            if e == PAIRED:
+                apply_silu(e - 1, raw3[:, :, :C])
+                hidden(e - 1)
+                if e - 1 in EARLY_W2:
+                    finish_group(EARLY_W2[e - 1], rounded2)
+            apply_silu(e, raw3[:, :, H - C :])
             if e in EARLY_W2:
                 rounded2 = round_group(EARLY_W2[e], raw2)
         w3_mx = quantize(rounded3[LAST][:], H, "w3", pieces=2)
@@ -277,6 +330,8 @@ def tile_moe_pkd_glu_silu_kernel(
             w2_mx[e] = (codes, scales[:])
             second_product(e)
 
+        for e in BETWEEN:
+            second_product(e)
         for e in raw_of:
             round_w2(e, raw_of[e], place[e])
             quantize_late(e)

@@ -26,24 +26,22 @@ PACK = 4
 LIST_ROWS = 16
 LAST = E - 1
 BURST = 256
-GATHER_EXPERTS = 3
-RING = 88 * 1024
-PAIRED = 10
-FIRST_SHARE = 48
-SLOT = H * PACK * 4 + C * PACK * 2
-H_OVERLAP = 32
+GATHERS = 4
+RAW = H * PACK * 4
+PAIRED = 12
+H_GROUPS = ((0, 1, 2, 3), (4, 5, 6, 7), (8, 9, 10, 11), (12, 13), (14, 15, 16, 17))
+LATE_W2 = ((0, 1, 2, 3), (4, 5, 6, 7), (8, 9, 10, 11), (12, 13), (14, 15), (16,), (17,))
+W2_ON_VECTOR = (7, 8, 12, 14, 16)
+LATE_BANKS = ((0, 1, 2, 3), (4, 5, 6, 7), (8, 9, 10, 11), (12, 13, 14, 15), (16, 17))
+Y_ON_VECTOR = (8, 12)
+RING = 96 * 1024
+W2_QUANTISED = ((0, 1, 2, 3), (4, 5, 6, 7), (8, 9, 10, 11), (12, 13), (14, 15), (16, 17))
+Y_BEHIND = 17
+W1_SHARE = 52
+Y_BANKS = 5
+SUM_BANKS = 3
+W2_BYTES = N * PACK * 2
 ROUNDED = H * PACK * 2
-ROUNDED_SLOTS = 12
-W1_SHARE = {LAST: 40}
-W3_SHARE = {10: 80, LAST - 1: 88, LAST: 48}
-EARLY_W2 = {5: (0, 1, 2, 3), 9: (4, 5, 6, 7), 12: (8, 9, 10, 11)}
-EARLY_BANKS = ((0, 1, 2, 3), (4, 5, 6, 7), (8, 9, 10, 11))
-BETWEEN = (12, 13)
-LATE_W2 = ((14, 15), (16, 17))
-W2_ON_VECTOR = (14,)
-LATE_BANKS = ((13, 14, 15, 16), (12, 17))
-Y_ON_VECTOR = (12,)
-WARM_PASSES = 4
 RANGE = 256
 FUSED = (2, 1, 1)
 
@@ -53,16 +51,24 @@ def tile_moe_pkd_glu_silu_kernel(
 ):
     nc = tc.nc
     with ExitStack() as ctx:
-        stream = ctx.enter_context(tc.tile_pool(name="stream", bufs=1))
-        rounds = ctx.enter_context(tc.tile_pool(name="rounds", bufs=1))
         keep = ctx.enter_context(tc.tile_pool(name="keep", bufs=1))
+        stream = ctx.enter_context(tc.tile_pool(name="stream", bufs=1))
+        late = ctx.enter_context(tc.tile_pool(name="late", bufs=1))
         work = ctx.enter_context(tc.tile_pool(name="work", bufs=2))
         psum = ctx.enter_context(tc.psum_pool(name="psum", bufs=2))
+        on_scalar, on_vector = nc.scalar.copy, nc.vector.tensor_copy
 
-        y = keep.tile([P, S], F32, name="y")
+        token_scales = keep.tile([P, T // 4], I32, name="token_scales", align_bytes=BURST)
+        nc.gpsimd.memset(token_scales[:], 0)
         identity = keep.tile([P, P], F32, name="identity")
         make_identity(nc, identity[:])
-        on_scalar, on_vector = nc.scalar.copy, nc.vector.tensor_copy
+
+        slot_words = keep.tile([P, S], U32, name="slot_words", align_bytes=64)
+        slot_scales = keep.tile([P, S], U8, name="slot_scales", align_bytes=64)
+        h_codes = keep.tile([P, S], U32, name="h_codes", align_bytes=64)
+        h_scales = keep.tile([P, S], U8, name="h_scales", align_bytes=64)
+        w2_codes = keep.tile([P, E * N], U32, name="w2_codes", align_bytes=64)
+        w2_scales = keep.tile([P, E * N], U8, name="w2_scales", align_bytes=64)
 
         ring = [0]
 
@@ -72,239 +78,187 @@ def tile_moe_pkd_glu_silu_kernel(
             ring.append(start + size)
             return stream.tile(shape, F32, name="raw%d" % len(ring), align_bytes=BURST, offset=start)
 
-        def load(weights, experts):
-            raw = ring_tile([P, len(experts), PACK, weights.shape[2]])
-            nc.sync.dma_start(
-                raw[:], weights[experts[0] : experts[-1] + 1].rearrange("g (p j) c -> p g j c", j=PACK)
-            )
+        def load(weights, first, count):
+            raw = ring_tile([P, count, PACK, weights.shape[2]])
+            nc.sync.dma_start(raw[:], weights[first : first + count].rearrange("g (p j) c -> p g j c", j=PACK))
             return raw
 
-        def rounded_start(e):
-            return e % ROUNDED_SLOTS * ROUNDED
-
-        def gather(g, slot):
-            width = GATHER_EXPERTS * C
+        def gather(g):
+            width = S // GATHERS
+            cols = slice(g * width, (g + 1) * width)
             offsets = slot_list[:, g * width // LIST_ROWS : (g + 1) * width // LIST_ROWS]
-            start = rounded_start(slot)
-            words = rounds.tile([P, width], U32, name="words%d" % g, align_bytes=64, offset=start)
-            scales = rounds.tile([P, width], U8, name="scales%d" % g, align_bytes=64, offset=start + 4 * width)
-            nc.vector.tensor_copy(words[:], token_words[:].bitcast(U32).indirect(offsets))
-            nc.vector.tensor_copy(scales[:], token_scales[:].bitcast(U8).indirect(offsets))
-            return words, scales
+            on_vector(slot_words[:, cols], token_words[:].bitcast(U32).indirect(offsets))
+            on_vector(slot_scales[:, cols], token_scales[:].bitcast(U8).indirect(offsets))
 
-        def quantize(rounded, width, name, bufs=2, pieces=1):
-            codes = work.tile([P, width], U32, name=name + "_codes", align_bytes=64, bufs=bufs)
-            scales = work.tile([P, width], U8, name=name + "_scales", align_bytes=64, bufs=bufs)
-            step = width // pieces
-            for c in range(0, width, step):
-                nc.vector.quantize_mx(
-                    out=codes[:, c : c + step].bitcast(FP8X4),
-                    scales=scales[:, c : c + step],
-                    in_=rounded[:, c * PACK : (c + step) * PACK],
-                )
-            return codes, scales
+        def quantize(codes, scales, rounded):
+            nc.vector.quantize_mx(out=codes.bitcast(FP8X4), scales=scales, in_=rounded)
 
-        def round_first(raw, rounded, share, pieces=1):
+        def rounded_tile(name, count, bufs):
+            return work.tile([P, count * H * PACK], BF16, name=name, align_bytes=64, bufs=bufs)
+
+        def round_one(copy, raw, rounded, first=0, last=P):
             dst = rounded.rearrange("p (t m u v) -> p m u t v", t=PACK, u=2, v=2)
             src = raw.rearrange("p (u v) (m t) -> p m u t v", t=PACK, u=2)
-            if share > 0:
-                on_scalar(dst[:, P - share :], src[:, P - share :])
-            if share < P:
-                for t in range(0, PACK, PACK // pieces):
-                    on_vector(
-                        dst[:, : P - share, :, t : t + PACK // pieces], src[:, : P - share, :, t : t + PACK // pieces]
+            copy(dst[:, first:last], src[:, first:last])
+
+        def round_pair(raw, rounded):
+            on_vector(
+                rounded.rearrange("p (g t m j) -> p g m t j", g=2, t=PACK, j=PACK),
+                raw.rearrange("p g j (m t) -> p g m t j", t=PACK),
+            )
+
+        def second_bank(e):
+            if e < LAST - 1:
+                return a[e]
+            return psum.tile([P, PACK, C], F32, name="y_acc", bufs=Y_BANKS)
+
+        def last_products(rounded, half):
+            codes = keep.tile([P, H // 2], U32, name="last_codes%d" % half, align_bytes=64)
+            scales = keep.tile([P, H // 2], U8, name="last_scales%d" % half, align_bytes=64)
+            quantize(codes[:], scales[:], rounded[:])
+            for t in range(2):
+                nc.tensor.matmul_mx(
+                    out=b[LAST][:, 2 * half + t, :],
+                    lhsT=codes[:, t * P : (t + 1) * P].bitcast(FP8X4),
+                    lhsT_scale=scales[:, t * P : (t + 1) * P],
+                    rhs=slot_words[:, LAST * C :].bitcast(FP8X4),
+                    rhs_scale=slot_scales[:, LAST * C :],
+                    start=True,
+                    stop=True,
+                )
+
+        def round_half(copy, raw, rounded, half):
+            src = raw.rearrange("p (u v) (m t) -> p m u t v", t=PACK, u=2)
+            copy(rounded.rearrange("p (t m u v) -> p m u t v", t=2, u=2, v=2), src[:, :, :, 2 * half : 2 * half + 2])
+
+        def first_products(rounded, first, count, name):
+            codes = work.tile([P, count * H], U32, name=name + "_codes", align_bytes=64)
+            scales = work.tile([P, count * H], U8, name=name + "_scales", align_bytes=64)
+            quantize(codes[:], scales[:], rounded[:])
+            for g in range(count):
+                slots = slice((first + g) * C, (first + g + 1) * C)
+                if name == "a":
+                    a[first + g] = psum.tile([P, PACK, C], F32, name="sums", bufs=SUM_BANKS)
+                else:
+                    b[first + g] = second_bank(first + g)
+                acc = (a if name == "a" else b)[first + g]
+                for t in range(PACK):
+                    cols = slice(g * H + t * P, g * H + (t + 1) * P)
+                    nc.tensor.matmul_mx(
+                        out=acc[:, t, :],
+                        lhsT=codes[:, cols].bitcast(FP8X4),
+                        lhsT_scale=scales[:, cols],
+                        rhs=slot_words[:, slots].bitcast(FP8X4),
+                        rhs_scale=slot_scales[:, slots],
+                        start=True,
+                        stop=True,
                     )
 
-        def first_product(weights, e, name):
-            words, scales = tokens[e // GATHER_EXPERTS]
-            cols = slice((e % GATHER_EXPERTS) * C, (e % GATHER_EXPERTS + 1) * C)
-            acc = psum.tile([P, PACK, C], F32, name=name)
-            for t in range(PACK):
-                nc.tensor.matmul_mx(
-                    out=acc[:, t, :],
-                    lhsT=weights[0][:, t * P : (t + 1) * P].bitcast(FP8X4),
-                    lhsT_scale=weights[1][:, t * P : (t + 1) * P],
-                    rhs=words[:, cols].bitcast(FP8X4),
-                    rhs_scale=scales[:, cols],
-                    start=True,
-                    stop=True,
-                )
-            return acc
-
-        def warm_up(weights):
-            words, scales = tokens[LAST // GATHER_EXPERTS]
-            for t in range(WARM_PASSES):
-                if t % 2 == 0:
-                    unread = psum.tile([P, 2, 2 * C], F32, name="unread")
-                nc.tensor.matmul_mx(
-                    out=unread[:, t % 2, :],
-                    lhsT=weights[0][:, t * P : (t + 1) * P].bitcast(FP8X4),
-                    lhsT_scale=weights[1][:, t * P : (t + 1) * P],
-                    rhs=words[:, : 2 * C].bitcast(FP8X4),
-                    rhs_scale=scales[:, : 2 * C],
-                    start=True,
-                    stop=True,
-                )
-
-        def multiply(e, h):
-            nc.vector.tensor_tensor(
-                h.rearrange("p (q c t) -> p q c t", q=PACK, t=PACK),
-                b[e][:].rearrange("p t (q c) -> p q c t", q=PACK),
-                silu_a[e],
-                MULT,
-            )
-
-        def round_w2(e, raw, rounded):
-            copy = on_vector if e in W2_ON_VECTOR else on_scalar
-            copy(
-                rounded.rearrange("p (m s u v) -> p m u s v", s=PACK, u=2, v=2),
-                raw.rearrange("p (u v) (m s) -> p m u s v", s=PACK, u=2),
-            )
-
-        def round_group(group, raw):
-            rounded = work.tile([P, len(group) * N * PACK], BF16, name="rounded2", align_bytes=64, bufs=1)
-            for g, e in enumerate(group):
-                round_w2(e, raw[:, g], rounded[:, g * N * PACK : (g + 1) * N * PACK])
-            return rounded
-
-        def quantize_group(group, rounded):
-            codes, scales = quantize(rounded, len(group) * N, "w2_%d" % group[0], 1)
-            for g, e in enumerate(group):
-                w2_mx[e] = (codes[:, g * N : (g + 1) * N], scales[:, g * N : (g + 1) * N])
-
-        def second_product(e):
-            bank = [x for x in EARLY_BANKS + LATE_BANKS if e in x][0]
-            if e == bank[0]:
-                banks[bank] = psum.tile([P, len(bank), C], F32, name="y_acc")
-            nc.tensor.matmul_mx(
-                out=banks[bank][:, bank.index(e), :],
-                lhsT=w2_mx[e][0].bitcast(FP8X4),
-                lhsT_scale=w2_mx[e][1],
-                rhs=h_mx[e][0][:].bitcast(FP8X4),
-                rhs_scale=h_mx[e][1][:],
-                start=True,
-                stop=True,
-            )
-            if e == bank[-1]:
-                copy = on_vector if bank[0] in Y_ON_VECTOR else on_scalar
-                copy(by_expert[:, bank[0] : e + 1 : bank[1] - bank[0], :], banks[bank][:])
-
-        banks = {}
-        by_expert = y[:].rearrange("p (e c) -> p e c", c=C)
-        tokens, b, silu_a, h_mx, w2_mx = {}, {}, {}, {}, {}
-        def load_w1(e):
-            slot1 = ring_tile([P, H * PACK])
-            nc.sync.dma_start(slot1[:, : H * PACK], w1[e].rearrange("(p j) c -> p (j c)", j=PACK))
-            return slot1
-
-        slot1 = load_w1(0)
-        slot_list = keep.tile([P, S // LIST_ROWS], U16, name="slot_list")
-        nc.sync.dma_start(slot_list[:], offs)
-        token_words = keep.tile([P, T], I32, name="token_words", align_bytes=BURST)
-        nc.sync.dma_start(token_words[:], x_words[0].rearrange("p t r -> p (t r)").bitcast(I32))
-        token_scales = keep.tile([P, T // 4], I32, name="token_scales")
-        loaded_scales = keep.tile([P, T // 4], I32, name="loaded_scales", align_bytes=BURST)
-        nc.vector.memset(token_scales[:], 0)
-        for quadrant in range(4):
-            nc.sync.dma_start(loaded_scales[quadrant:P:32, :], x_scales[0, quadrant:16:4, :].bitcast(I32))
-        for quadrant in range(4):
-            rows = slice(32 * quadrant, 32 * quadrant + 4)
-            nc.vector.tensor_copy(token_scales[rows, :], loaded_scales[rows, :])
-
-        def rounded_tile(e, count):
-            return rounds.tile(
-                [P, count * H * PACK], BF16, name="rounded1_%d" % e, align_bytes=64, offset=rounded_start(e)
-            )
+        a, b, silu_a, h = {}, {}, {}, {}
 
         def apply_silu(e, place):
             silu_a[e] = place.rearrange("p q (c t) -> p q c t", t=PACK)
             nc.scalar.activation(silu_a[e], a[e][:].rearrange("p t (q c) -> p q c t", q=PACK), SILU)
 
-        def hidden(e):
-            h = work.tile([P, C * PACK], BF16, name="h", align_bytes=64)
-            multiply(e, h[:])
-            h_mx[e] = quantize(h[:], C, "h", bufs=E)
+        def multiply(e):
+            group = [x for x in H_GROUPS if e in x][0]
+            if e == group[0]:
+                h[group] = work.tile([P, len(group), C, PACK], BF16, name="h", align_bytes=64)
+            nc.vector.tensor_tensor(
+                h[group][:, e - group[0]].rearrange("p (q c) t -> p q c t", q=PACK),
+                b[e][:].rearrange("p t (q c) -> p q c t", q=PACK),
+                silu_a[e],
+                MULT,
+            )
 
-        def halves(mx):
-            return [(mx[0][:, g * H : (g + 1) * H], mx[1][:, g * H : (g + 1) * H]) for g in range(2)]
+        def quantize_h(group):
+            cols = slice(group[0] * C, (group[-1] + 1) * C)
+            quantize(h_codes[:, cols], h_scales[:, cols], h[group][:].rearrange("p g c t -> p (g c t)"))
 
-        def finish_group(group, rounded):
-            quantize_group(group, rounded[:])
-            for x in group:
-                second_product(x)
+        def finish_h(e):
+            for group in H_GROUPS:
+                if e == group[-1]:
+                    quantize_h(group)
 
-        for g, slot in enumerate((7, 9, 11)):
-            tokens[g] = gather(g, slot)
-        a, rounded3 = {}, {}
-        rounded1 = rounded_tile(0, 1)
-        round_first(slot1[:, : H * PACK].rearrange("p (j c) -> p j c", j=PACK), rounded1[:], 0)
-        a[0] = first_product(quantize(rounded1[:], H, "w1"), 0, "a")
-        for e in range(0, PAIRED, 2):
-            pair3 = load(w3, (e, e + 1))
-            both = work.tile([P, 2 * H * PACK], BF16, name="rounded3", align_bytes=64)
-            round_first(pair3[:, 0], both[:, : H * PACK], FIRST_SHARE)
-            round_first(pair3[:, 1], both[:, H * PACK :], P)
+        def round_w2(group, raw, rounded):
+            for g, e in enumerate(group):
+                copy = on_vector if e in W2_ON_VECTOR else on_scalar
+                copy(
+                    rounded[:, g].rearrange("p (m s u v) -> p m u s v", s=PACK, u=2, v=2),
+                    raw[:, g].rearrange("p (u v) (m s) -> p m u s v", s=PACK, u=2),
+                )
+
+        def quantize_w2(group, rounded):
+            cols = slice(group[0] * N, (group[-1] + 1) * N)
+            quantize(w2_codes[:, cols], w2_scales[:, cols], rounded.rearrange("p g x -> p (g x)"))
+
+        def second_products(bank):
+            acc = psum.tile([P, len(bank), C], F32, name="y_acc", bufs=Y_BANKS)
+            for g, e in enumerate(bank):
+                cols = slice(e * C, (e + 1) * C)
+                nc.tensor.matmul_mx(
+                    out=acc[:, g, :],
+                    lhsT=w2_codes[:, cols].bitcast(FP8X4),
+                    lhsT_scale=w2_scales[:, cols],
+                    rhs=h_codes[:, cols].bitcast(FP8X4),
+                    rhs_scale=h_scales[:, cols],
+                    start=True,
+                    stop=True,
+                )
+            copy = on_vector if bank[0] in Y_ON_VECTOR else on_scalar
+            copy(y[:, bank[0] * C : (bank[-1] + 1) * C], acc[:].rearrange("p g c -> p (g c)"))
+
+        def silu_tile(e):
+            place = work.tile([P, PACK, C], F32, name="silu_a", bufs=3)
+            apply_silu(e, place[:])
+
+        token_words = keep.tile([P, T], I32, name="token_words", align_bytes=BURST)
+        nc.sync.dma_start(token_words[:], x_words[0].rearrange("p t r -> p (t r)").bitcast(I32))
+        slot_list = keep.tile([P, S // LIST_ROWS], U16, name="slot_list")
+        nc.sync.dma_start(slot_list[:], offs)
+        raw3 = load(w3, 0, 2)
+        for row in range(4):
+            nc.sync.dma_start(token_scales[row:P:32, :], x_scales[0, row:16:4, :].bitcast(I32))
+        gather(0)
+        steps = [(e, e + 1) for e in range(0, PAIRED, 2)] + [(e,) for e in range(PAIRED, E)]
+        rounded3 = None
+        for s, step in enumerate(steps):
+            e, count = step[0], len(step)
+            before = steps[s - 1] if s > 0 else ()
+            raw1 = load(w1, e, count)
             if e > 0:
-                apply_silu(e - 1, pair3[:, 0, :, :C])
-            apply_silu(e, pair3[:, 0, :, H - C :])
-            if e > 0:
-                hidden(e - 1)
-            for g, mx in enumerate(halves(quantize(both[:], 2 * H, "w3"))):
-                b[e + g] = first_product(mx, e + g, "b")
-            if e - 1 in EARLY_W2:
-                finish_group(EARLY_W2[e - 1], rounded2)
-            pair1 = load(w1, (e + 1, e + 2))
-            if e + 1 in EARLY_W2:
-                raw2 = load(w2, EARLY_W2[e + 1])
-            both = rounded_tile(e + 1, 2)
-            round_first(pair1[:, 0], both[:, : H * PACK], 0)
-            round_first(pair1[:, 1], both[:, H * PACK :], P)
-            hidden(e)
-            for g, mx in enumerate(halves(quantize(both[:], 2 * H, "w1"))):
-                a[e + 1 + g] = first_product(mx, e + 1 + g, "a")
-            if e // 2 + 3 < E // GATHER_EXPERTS:
-                tokens[e // 2 + 3] = gather(e // 2 + 3, e + 2)
-            if e + 1 in EARLY_W2:
-                rounded2 = round_group(EARLY_W2[e + 1], raw2)
-        for e in range(PAIRED, E):
-            if e > PAIRED:
-                slot1 = load_w1(e)
+                raw3 = load(w3, e, count)
+            rounded1 = rounded_tile("rounded1", count, 2)
+            if before:
+                first_products(rounded3, before[0], len(before), "b")
+            if count == 2:
+                round_pair(raw1[:], rounded1[:])
+            elif e == LAST:
+                round_one(on_scalar, raw1[:, 0], rounded1[:], 0, W1_SHARE)
+                round_one(on_vector, raw1[:, 0], rounded1[:], W1_SHARE, P)
+            else:
+                round_one(on_vector, raw1[:, 0], rounded1[:])
             if e == LAST:
-                raw_between = load(w2, BETWEEN)
-            raw3 = load(w3, (e,))[:, 0]
-            if e in EARLY_W2:
-                raw2 = load(w2, EARLY_W2[e])
-            if e > PAIRED:
-                rounded1 = rounded_tile(e, 1)
-                raw1 = slot1[:, : H * PACK].rearrange("p (j c) -> p j c", j=PACK)
-                round_first(raw1, rounded1[:], W1_SHARE.get(e, 0))
-                b[e - 1] = first_product(quantize(rounded3[e - 1][:], H, "w3"), e - 1, "b")
-                h = slot1[:, : C * PACK // 2].bitcast(BF16)
-                w1_mx = quantize(rounded1[:], H, "w1")
-                a[e] = first_product(w1_mx, e, "a")
-                multiply(e - 1, h)
-                if e == LAST:
-                    warm_up(w1_mx)
-                h_mx[e - 1] = quantize(h, C, "h", bufs=E)
-                if e - 1 in EARLY_W2:
-                    finish_group(EARLY_W2[e - 1], rounded2)
-            if e == LAST:
-                quantize_group(BETWEEN, round_group(BETWEEN, raw_between)[:])
-            rounded3[e] = work.tile([P, H * PACK], BF16, name="rounded3", align_bytes=64)
-            round_first(raw3, rounded3[e][:], W3_SHARE.get(e, P), pieces=2 if e == LAST else 1)
-            if e == PAIRED:
-                apply_silu(e - 1, raw3[:, :, :C])
-                hidden(e - 1)
-                if e - 1 in EARLY_W2:
-                    finish_group(EARLY_W2[e - 1], rounded2)
-            apply_silu(e, raw3[:, :, H - C :])
-            if e in EARLY_W2:
-                rounded2 = round_group(EARLY_W2[e], raw2)
-        w3_mx = quantize(rounded3[LAST][:], H, "w3", pieces=2)
-        b[LAST] = first_product(w3_mx, LAST, "b")
-        warm_up(w3_mx)
-
-        late_raw = {group: load(w2, group) for group in LATE_W2}
+                first_products(rounded1, e, count, "a")
+                break
+            for x in before:
+                multiply(x)
+            first_products(rounded1, e, count, "a")
+            finish_h(e - 1)
+            rounded3 = rounded_tile("rounded3", count, 2)
+            for g in range(count):
+                round_one(on_scalar, raw3[:, g], rounded3[:, g * H * PACK : (g + 1) * H * PACK])
+            for x in step:
+                if x < LAST - 1:
+                    silu_tile(x)
+            if s + 1 < GATHERS:
+                gather(s + 1)
+        late_raw = {}
+        for group in LATE_W2:
+            late_raw[group] = load(w2, group[0], len(group))
+            if group[0] == Y_BEHIND:
+                y = stream.tile([P, S], F32, name="y", align_bytes=BURST, offset=ring[-1] - BURST)
+                ring.append(ring[-1] - BURST + 4 * S)
         back_lists = []
         for r, pos in enumerate((pos1, pos2, pos3)):
             back = keep.tile([P, T // LIST_ROWS], U16, name="back_list%d" % r)
@@ -315,44 +269,43 @@ def tile_moe_pkd_glu_silu_kernel(
             gates[t0] = ring_tile([P, TOP, RANGE])
             nc.sync.dma_start(gates[t0][:], gate[:, :, t0 : t0 + RANGE].rearrange("r p t -> p r t"))
 
-        last_h = keep.tile([P, C * PACK], BF16, name="last_h", align_bytes=64)
-        multiply(LAST, last_h[:])
-        h_mx[LAST] = quantize(last_h[:], C, "h", bufs=E)
-
-        raw_of = {e: late_raw[group][:, g] for group in LATE_W2 for g, e in enumerate(group)}
-        width = N * PACK
-        place = {e: keep.tile([P, width], BF16, name="late_rounded%d" % e, align_bytes=64)[:] for e in raw_of}
-
-        def quantize_late(e):
-            codes = keep.tile([P, N], U32, name="late_codes%d" % e, align_bytes=64)[:]
-            scales = keep.tile([P, N], U8, name="late_scales%d" % e, align_bytes=64)
-            nc.vector.quantize_mx(out=codes.bitcast(FP8X4), scales=scales[:], in_=place[e])
-            w2_mx[e] = (codes, scales[:])
-            second_product(e)
-
-        for e in BETWEEN:
-            second_product(e)
-        for e in raw_of:
-            round_w2(e, raw_of[e], place[e])
-            quantize_late(e)
+        halves = [keep.tile([P, H * PACK // 2], BF16, name="last_w3_%d" % g, align_bytes=64) for g in range(2)]
+        round_half(on_scalar, raw3[:, 0], halves[1][:], 1)
+        round_half(on_vector, raw3[:, 0], halves[0][:], 0)
+        apply_silu(LAST - 1, raw3[:, 0, :, :C])
+        apply_silu(LAST, raw3[:, 0, :, H - C :])
+        b[LAST] = second_bank(LAST)
+        last_products(halves[1], 1)
+        last_products(halves[0], 0)
+        multiply(LAST - 1)
+        multiply(LAST)
+        finish_h(LAST)
+        rounded2 = late.tile([P, E, N * PACK], BF16, name="rounded2", align_bytes=BURST, offset=0)
+        for group in LATE_W2:
+            round_w2(group, late_raw[group], rounded2[:, group[0] : group[-1] + 1])
+            for joint in W2_QUANTISED:
+                if joint[-1] == group[-1]:
+                    quantize_w2(joint, rounded2[:, joint[0] : joint[-1] + 1])
+        for bank in LATE_BANKS:
+            second_products(bank)
 
         spare = []
 
         def spare_tile(width):
             start = sum(spare)
             spare.append(4 * RANGE)
-            return rounds.tile([P, width], F32, name="spare%d" % len(spare), align_bytes=BURST, offset=start)
+            return late.tile([P, width], F32, name="spare%d" % len(spare), align_bytes=BURST, offset=start)
 
         def looked_up(r, t0):
             return y[:].indirect(back_lists[r][:, t0 // LIST_ROWS : (t0 + RANGE) // LIST_ROWS])
 
-        early, middle, late = range(0, T, RANGE)
+        early, middle, final = range(0, T, RANGE)
         plain, parts = {}, {}
-        for t0, fused in zip((early, middle, late), FUSED):
+        for t0, fused in zip((early, middle, final), FUSED):
             for r in range(fused, TOP):
                 plain[r, t0] = spare_tile(RANGE)
                 nc.scalar.activation(plain[r, t0][:], looked_up(r, t0), COPY)
-        for t0 in (early, middle, late):
+        for t0 in (early, middle, final):
             for r in range(TOP):
                 parts[r, t0] = spare_tile(RANGE)
                 fetched = plain[r, t0][:] if (r, t0) in plain else looked_up(r, t0)
@@ -361,7 +314,7 @@ def tile_moe_pkd_glu_silu_kernel(
         blocks = RANGE // P
         sums, back_turned = {}, {}
         for t0 in (early, middle):
-            sums[t0] = [psum.tile([P, P], F32, name="ab"[blk]) for blk in range(blocks)]
+            sums[t0] = [psum.tile([P, P], F32, name="y_acc", bufs=Y_BANKS) for blk in range(blocks)]
             for r in range(TOP):
                 for blk in range(blocks):
                     nc.tensor.matmul(
@@ -369,7 +322,7 @@ def tile_moe_pkd_glu_silu_kernel(
                         start=r == 0, stop=r == TOP - 1, is_transpose=True,
                     )
         for t0 in (early, middle):
-            back_turned[t0] = psum.tile([P, blocks, P], F32, name="y_acc")
+            back_turned[t0] = psum.tile([P, blocks, P], F32, name="sums", bufs=SUM_BANKS)
             for blk in range(blocks):
                 turned = keep.tile([P, P], F32, name="turned%d_%d" % (t0, blk))
                 on_scalar(turned[:], sums[t0][blk][:])
@@ -381,8 +334,8 @@ def tile_moe_pkd_glu_silu_kernel(
 
         pair = spare_tile(RANGE)
         rest = spare_tile(RANGE)
-        for total, first, second in ((pair, parts[0, late], parts[1, late]), (rest, pair, parts[2, late])):
+        for total, first, second in ((pair, parts[0, final], parts[1, final]), (rest, pair, parts[2, final])):
             for blk in range(blocks):
                 cols = slice(blk * P, (blk + 1) * P)
                 nc.vector.tensor_tensor(total[:, cols], first[:, cols], second[:, cols], ADD)
-        nc.sync.dma_start(out[:, late:], rest[:])
+        nc.sync.dma_start(out[:, final:], rest[:])

import math
from contextlib import ExitStack

import concourse.mybir as mybir
from concourse.masks import make_identity

K, T, E, C, H, N = 512, 768, 18, 128, 512, 128
TOP = 3
S = E * C
FLOPS = 2 * S * (2 * K * H + H * N)

F32 = mybir.dt.float32
BF16 = mybir.dt.bfloat16
I32 = mybir.dt.int32
U32 = mybir.dt.uint32
U16 = mybir.dt.uint16
U8 = mybir.dt.uint8
FP8X4 = mybir.dt.float8_e4m3fn_x4
MULT = mybir.AluOpType.mult
ADD = mybir.AluOpType.add
SILU = mybir.ActivationFunctionType.Silu
COPY = mybir.ActivationFunctionType.Copy

P = 128
PACK = 4
LIST_ROWS = 16
LAST = E - 1
BURST = 256
GATHERS = 4
RAW = H * PACK * 4
PAIRED = 12
H_GROUPS = ((0, 1, 2, 3), (4, 5, 6, 7), (8, 9, 10, 11), (12, 13), (14, 15, 16, 17))
LATE_W2 = ((0, 1, 2, 3), (4, 5, 6, 7), (8, 9, 10, 11), (12, 13), (14, 15), (16,), (17,))
W2_ON_VECTOR = (7, 8, 12, 14, 16)
LATE_BANKS = ((0, 1, 2, 3), (4, 5, 6, 7), (8, 9, 10, 11), (12, 13, 14, 15), (16, 17))
Y_ON_VECTOR = (8, 12)
RING = 96 * 1024
W2_QUANTISED = ((0, 1, 2, 3), (4, 5, 6, 7), (8, 9, 10, 11), (12, 13), (14, 15), (16, 17))
Y_BEHIND = 17
W1_SHARE = 52
Y_BANKS = 5
SUM_BANKS = 3
W2_BYTES = N * PACK * 2
ROUNDED = H * PACK * 2
RANGE = 256
FUSED = (2, 1, 1)


def tile_moe_pkd_glu_silu_kernel(
    tc, x_words, x_scales, w1, w3, w2, gate, offs, pos1, pos2, pos3, out
):
    nc = tc.nc
    with ExitStack() as ctx:
        keep = ctx.enter_context(tc.tile_pool(name="keep", bufs=1))
        stream = ctx.enter_context(tc.tile_pool(name="stream", bufs=1))
        late = ctx.enter_context(tc.tile_pool(name="late", bufs=1))
        work = ctx.enter_context(tc.tile_pool(name="work", bufs=2))
        psum = ctx.enter_context(tc.psum_pool(name="psum", bufs=2))
        on_scalar, on_vector = nc.scalar.copy, nc.vector.tensor_copy

        token_scales = keep.tile([P, T // 4], I32, name="token_scales", align_bytes=BURST)
        nc.gpsimd.memset(token_scales[:], 0)
        identity = keep.tile([P, P], F32, name="identity")
        make_identity(nc, identity[:])

        slot_words = keep.tile([P, S], U32, name="slot_words", align_bytes=64)
        slot_scales = keep.tile([P, S], U8, name="slot_scales", align_bytes=64)
        h_codes = keep.tile([P, S], U32, name="h_codes", align_bytes=64)
        h_scales = keep.tile([P, S], U8, name="h_scales", align_bytes=64)
        w2_codes = keep.tile([P, E * N], U32, name="w2_codes", align_bytes=64)
        w2_scales = keep.tile([P, E * N], U8, name="w2_scales", align_bytes=64)

        ring = [0]

        def ring_tile(shape):
            size = 4 * math.prod(shape[1:])
            start = ring[-1] if ring[-1] + size <= RING else 0
            ring.append(start + size)
            return stream.tile(shape, F32, name="raw%d" % len(ring), align_bytes=BURST, offset=start)

        def load(weights, first, count):
            raw = ring_tile([P, count, PACK, weights.shape[2]])
            nc.sync.dma_start(raw[:], weights[first : first + count].rearrange("g (p j) c -> p g j c", j=PACK))
            return raw

        def gather(g):
            width = S // GATHERS
            cols = slice(g * width, (g + 1) * width)
            offsets = slot_list[:, g * width // LIST_ROWS : (g + 1) * width // LIST_ROWS]
            on_vector(slot_words[:, cols], token_words[:].bitcast(U32).indirect(offsets))
            on_vector(slot_scales[:, cols], token_scales[:].bitcast(U8).indirect(offsets))

        def quantize(codes, scales, rounded):
            nc.vector.quantize_mx(out=codes.bitcast(FP8X4), scales=scales, in_=rounded)

        def rounded_tile(name, count, bufs):
            return work.tile([P, count * H * PACK], BF16, name=name, align_bytes=64, bufs=bufs)

        def round_one(copy, raw, rounded, first=0, last=P):
            dst = rounded.rearrange("p (t m u v) -> p m u t v", t=PACK, u=2, v=2)
            src = raw.rearrange("p (u v) (m t) -> p m u t v", t=PACK, u=2)
            copy(dst[:, first:last], src[:, first:last])

        def round_pair(raw, rounded):
            on_vector(
                rounded.rearrange("p (g t m j) -> p g m t j", g=2, t=PACK, j=PACK),
                raw.rearrange("p g j (m t) -> p g m t j", t=PACK),
            )

        def second_bank(e):
            if e < LAST - 1:
                return a[e]
            return psum.tile([P, PACK, C], F32, name="y_acc", bufs=Y_BANKS)

        def last_products(rounded, half):
            codes = keep.tile([P, H // 2], U32, name="last_codes%d" % half, align_bytes=64)
            scales = keep.tile([P, H // 2], U8, name="last_scales%d" % half, align_bytes=64)
            quantize(codes[:], scales[:], rounded[:])
            for t in range(2):
                nc.tensor.matmul_mx(
                    out=b[LAST][:, 2 * half + t, :],
                    lhsT=codes[:, t * P : (t + 1) * P].bitcast(FP8X4),
                    lhsT_scale=scales[:, t * P : (t + 1) * P],
                    rhs=slot_words[:, LAST * C :].bitcast(FP8X4),
                    rhs_scale=slot_scales[:, LAST * C :],
                    start=True,
                    stop=True,
                )

        def round_half(copy, raw, rounded, half):
            src = raw.rearrange("p (u v) (m t) -> p m u t v", t=PACK, u=2)
            copy(rounded.rearrange("p (t m u v) -> p m u t v", t=2, u=2, v=2), src[:, :, :, 2 * half : 2 * half + 2])

        def first_products(rounded, first, count, name):
            codes = work.tile([P, count * H], U32, name=name + "_codes", align_bytes=64)
            scales = work.tile([P, count * H], U8, name=name + "_scales", align_bytes=64)
            quantize(codes[:], scales[:], rounded[:])
            for g in range(count):
                slots = slice((first + g) * C, (first + g + 1) * C)
                if name == "a":
                    a[first + g] = psum.tile([P, PACK, C], F32, name="sums", bufs=SUM_BANKS)
                else:
                    b[first + g] = second_bank(first + g)
                acc = (a if name == "a" else b)[first + g]
                for t in range(PACK):
                    cols = slice(g * H + t * P, g * H + (t + 1) * P)
                    nc.tensor.matmul_mx(
                        out=acc[:, t, :],
                        lhsT=codes[:, cols].bitcast(FP8X4),
                        lhsT_scale=scales[:, cols],
                        rhs=slot_words[:, slots].bitcast(FP8X4),
                        rhs_scale=slot_scales[:, slots],
                        start=True,
                        stop=True,
                    )

        a, b, silu_a, h = {}, {}, {}, {}

        def apply_silu(e, place):
            silu_a[e] = place.rearrange("p q (c t) -> p q c t", t=PACK)
            nc.scalar.activation(silu_a[e], a[e][:].rearrange("p t (q c) -> p q c t", q=PACK), SILU)

        def multiply(e):
            group = [x for x in H_GROUPS if e in x][0]
            if e == group[0]:
                h[group] = work.tile([P, len(group), C, PACK], BF16, name="h", align_bytes=64)
            nc.vector.tensor_tensor(
                h[group][:, e - group[0]].rearrange("p (q c) t -> p q c t", q=PACK),
                b[e][:].rearrange("p t (q c) -> p q c t", q=PACK),
                silu_a[e],
                MULT,
            )

        def quantize_h(group):
            cols = slice(group[0] * C, (group[-1] + 1) * C)
            quantize(h_codes[:, cols], h_scales[:, cols], h[group][:].rearrange("p g c t -> p (g c t)"))

        def finish_h(e):
            for group in H_GROUPS:
                if e == group[-1]:
                    quantize_h(group)

        def round_w2(group, raw, rounded):
            for g, e in enumerate(group):
                copy = on_vector if e in W2_ON_VECTOR else on_scalar
                copy(
                    rounded[:, g].rearrange("p (m s u v) -> p m u s v", s=PACK, u=2, v=2),
                    raw[:, g].rearrange("p (u v) (m s) -> p m u s v", s=PACK, u=2),
                )

        def quantize_w2(group, rounded):
            cols = slice(group[0] * N, (group[-1] + 1) * N)
            quantize(w2_codes[:, cols], w2_scales[:, cols], rounded.rearrange("p g x -> p (g x)"))

        def second_products(bank):
            acc = psum.tile([P, len(bank), C], F32, name="y_acc", bufs=Y_BANKS)
            for g, e in enumerate(bank):
                cols = slice(e * C, (e + 1) * C)
                nc.tensor.matmul_mx(
                    out=acc[:, g, :],
                    lhsT=w2_codes[:, cols].bitcast(FP8X4),
                    lhsT_scale=w2_scales[:, cols],
                    rhs=h_codes[:, cols].bitcast(FP8X4),
                    rhs_scale=h_scales[:, cols],
                    start=True,
                    stop=True,
                )
            copy = on_vector if bank[0] in Y_ON_VECTOR else on_scalar
            copy(y[:, bank[0] * C : (bank[-1] + 1) * C], acc[:].rearrange("p g c -> p (g c)"))

        def silu_tile(e):
            place = work.tile([P, PACK, C], F32, name="silu_a", bufs=3)
            apply_silu(e, place[:])

        token_words = keep.tile([P, T], I32, name="token_words", align_bytes=BURST)
        nc.sync.dma_start(token_words[:], x_words[0].rearrange("p t r -> p (t r)").bitcast(I32))
        slot_list = keep.tile([P, S // LIST_ROWS], U16, name="slot_list")
        nc.sync.dma_start(slot_list[:], offs)
        raw3 = load(w3, 0, 2)
        for row in range(4):
            nc.sync.dma_start(token_scales[row:P:32, :], x_scales[0, row:16:4, :].bitcast(I32))
        gather(0)
        steps = [(e, e + 1) for e in range(0, PAIRED, 2)] + [(e,) for e in range(PAIRED, E)]
        rounded3 = None
        for s, step in enumerate(steps):
            e, count = step[0], len(step)
            before = steps[s - 1] if s > 0 else ()
            raw1 = load(w1, e, count)
            if e > 0:
                raw3 = load(w3, e, count)
            rounded1 = rounded_tile("rounded1", count, 2)
            if before:
                first_products(rounded3, before[0], len(before), "b")
            if count == 2:
                round_pair(raw1[:], rounded1[:])
            elif e == LAST:
                round_one(on_scalar, raw1[:, 0], rounded1[:], 0, W1_SHARE)
                round_one(on_vector, raw1[:, 0], rounded1[:], W1_SHARE, P)
            else:
                round_one(on_vector, raw1[:, 0], rounded1[:])
            if e == LAST:
                first_products(rounded1, e, count, "a")
                break
            for x in before:
                multiply(x)
            first_products(rounded1, e, count, "a")
            finish_h(e - 1)
            rounded3 = rounded_tile("rounded3", count, 2)
            for g in range(count):
                round_one(on_scalar, raw3[:, g], rounded3[:, g * H * PACK : (g + 1) * H * PACK])
            for x in step:
                if x < LAST - 1:
                    silu_tile(x)
            if s + 1 < GATHERS:
                gather(s + 1)
        late_raw = {}
        for group in LATE_W2:
            late_raw[group] = load(w2, group[0], len(group))
            if group[0] == Y_BEHIND:
                y = stream.tile([P, S], F32, name="y", align_bytes=BURST, offset=ring[-1] - BURST)
                ring.append(ring[-1] - BURST + 4 * S)
        back_lists = []
        for r, pos in enumerate((pos1, pos2, pos3)):
            back = keep.tile([P, T // LIST_ROWS], U16, name="back_list%d" % r)
            nc.sync.dma_start(back[:], pos)
            back_lists.append(back)
        gates = {}
        for t0 in range(0, T, RANGE):
            gates[t0] = ring_tile([P, TOP, RANGE])
            nc.sync.dma_start(gates[t0][:], gate[:, :, t0 : t0 + RANGE].rearrange("r p t -> p r t"))

        halves = [keep.tile([P, H * PACK // 2], BF16, name="last_w3_%d" % g, align_bytes=64) for g in range(2)]
        round_half(on_scalar, raw3[:, 0], halves[1][:], 1)
        round_half(on_vector, raw3[:, 0], halves[0][:], 0)
        apply_silu(LAST - 1, raw3[:, 0, :, :C])
        apply_silu(LAST, raw3[:, 0, :, H - C :])
        b[LAST] = second_bank(LAST)
        last_products(halves[1], 1)
        last_products(halves[0], 0)
        multiply(LAST - 1)
        multiply(LAST)
        finish_h(LAST)
        rounded2 = late.tile([P, E, N * PACK], BF16, name="rounded2", align_bytes=BURST, offset=0)
        for group in LATE_W2:
            round_w2(group, late_raw[group], rounded2[:, group[0] : group[-1] + 1])
            for joint in W2_QUANTISED:
                if joint[-1] == group[-1]:
                    quantize_w2(joint, rounded2[:, joint[0] : joint[-1] + 1])
        for bank in LATE_BANKS:
            second_products(bank)

        spare = []

        def spare_tile(width):
            start = sum(spare)
            spare.append(4 * RANGE)
            return late.tile([P, width], F32, name="spare%d" % len(spare), align_bytes=BURST, offset=start)

        def looked_up(r, t0):
            return y[:].indirect(back_lists[r][:, t0 // LIST_ROWS : (t0 + RANGE) // LIST_ROWS])

        early, middle, final = range(0, T, RANGE)
        plain, parts = {}, {}
        for t0, fused in zip((early, middle, final), FUSED):
            for r in range(fused, TOP):
                plain[r, t0] = spare_tile(RANGE)
                nc.scalar.activation(plain[r, t0][:], looked_up(r, t0), COPY)
        for t0 in (early, middle, final):
            for r in range(TOP):
                parts[r, t0] = spare_tile(RANGE)
                fetched = plain[r, t0][:] if (r, t0) in plain else looked_up(r, t0)
                nc.vector.tensor_tensor(parts[r, t0][:], fetched, gates[t0][:, r, :], MULT)

        blocks = RANGE // P
        sums, back_turned = {}, {}
        for t0 in (early, middle):
            sums[t0] = [psum.tile([P, P], F32, name="y_acc", bufs=Y_BANKS) for blk in range(blocks)]
            for r in range(TOP):
                for blk in range(blocks):
                    nc.tensor.matmul(
                        sums[t0][blk][:], parts[r, t0][:, blk * P : (blk + 1) * P], identity[:],
                        start=r == 0, stop=r == TOP - 1, is_transpose=True,
                    )
        for t0 in (early, middle):
            back_turned[t0] = psum.tile([P, blocks, P], F32, name="sums", bufs=SUM_BANKS)
            for blk in range(blocks):
                turned = keep.tile([P, P], F32, name="turned%d_%d" % (t0, blk))
                on_scalar(turned[:], sums[t0][blk][:])
                nc.tensor.transpose(back_turned[t0][:, blk, :], turned[:], identity[:])
        for t0, queue in ((early, nc.sync), (middle, nc.scalar)):
            head = spare_tile(RANGE)
            on_scalar(head[:], back_turned[t0][:].rearrange("p blk c -> p (blk c)"))
            queue.dma_start(out[:, t0 : t0 + RANGE], head[:])

        pair = spare_tile(RANGE)
        rest = spare_tile(RANGE)
        for total, first, second in ((pair, parts[0, final], parts[1, final]), (rest, pair, parts[2, final])):
            for blk in range(blocks):
                cols = slice(blk * P, (blk + 1) * P)
                nc.vector.tensor_tensor(total[:, cols], first[:, cols], second[:, cols], ADD)
        nc.sync.dma_start(out[:, final:], rest[:])
